import numpy as np
import ml_dtypes


def mxq(x, axis, fmt="e4m3"):
    dtype, down = {"e4m3": (ml_dtypes.float8_e4m3fn, 7), "e5m2": (ml_dtypes.float8_e5m2, 14)}[fmt]
    v = np.moveaxis(np.asarray(x, np.float32).astype(ml_dtypes.bfloat16).astype(np.float64), axis, -1)
    blocks = v.reshape(v.shape[:-1] + (-1, 32))
    amax = np.abs(blocks).max(-1, keepdims=True)
    byte = np.maximum(np.where(amax > 0, np.frexp(amax)[1] - 1 + 127, 0) - down, 1)
    scale = np.exp2(byte - 127.0)
    codes = (blocks / scale).astype(np.float32).astype(dtype).astype(np.float64)
    return np.moveaxis((codes * scale).reshape(v.shape), -1, axis)


WIDE = False


def mx_kscale(k):
    if not WIDE:
        return np.ones(k)
    levels = np.array([10, -10, 5, -5, 0])
    if k % 512:
        return np.exp2(np.random.permutation(np.resize(levels, k // 32))).repeat(32)
    a = np.empty((k // 512, 16))
    for p in range(k // 512):
        a[p, :8] = np.random.permutation(np.resize(levels, 8))
        for g in range(8):
            far = levels[np.abs(levels - a[p, g]) >= 10]
            a[p, g + 8] = far[np.random.randint(len(far))]
    return np.exp2(a.ravel()).repeat(32)


def f64(x):
    return np.asarray(x).astype(np.float64)


def striped(idx):
    return np.tile(idx.reshape(-1, 16).T, (8, 1)).astype(np.uint16)


def unstriped(offs):
    return offs[:16].T.reshape(-1).astype(np.int64)


E2M1 = np.array([0.0, 0.5, 1.0, 1.5, 2.0, 3.0, 4.0, 6.0, -0.0, -0.5, -1.0, -1.5, -2.0, -3.0, -4.0, -6.0])


def pack_fp4(w):
    k, n = w.shape
    w = f64(np.asarray(w, np.float32).astype(ml_dtypes.bfloat16)).reshape(k // 32, 32, n)
    amax = np.abs(w).max(1)
    mant, ex = np.frexp(amax / 6.0)
    byte = np.clip(np.where(amax > 0, np.where(mant > 0.5, ex, ex - 1) + 127, 1), 1, 254)
    scaled = (w * np.exp2(127.0 - byte)[:, None, :]).reshape(k, n).astype(np.float32)
    c = np.ascontiguousarray(scaled.reshape(k // 512, 128, 4, n).transpose(0, 1, 3, 2)).astype(ml_dtypes.float4_e2m1fn).view(np.uint8) & 0xF
    words = (c[..., 0::2] | (c[..., 1::2] << 4)).reshape(k // 512, 128, 2 * n)
    return np.ascontiguousarray(words), np.ascontiguousarray(byte.astype(np.uint8).reshape(k // 512, 16, n))


def unpack_fp4(words, scales):
    g, _, n = scales.shape
    words = np.ascontiguousarray(words).reshape(g, 128, n, 2)
    nib = np.empty((g, 128, n, 4), np.uint8)
    nib[..., 0::2] = words & 0xF
    nib[..., 1::2] = words >> 4
    vals = E2M1[nib] * np.repeat(np.exp2(scales.astype(np.float64) - 127.0), 8, axis=1)[..., None]
    return vals.transpose(0, 1, 3, 2).reshape(g * 512, n)


def relu(v):
    return np.maximum(v, 0.0)


K, T, S, D, V, N = 512, 2048, 1024, 2, 512, 256
P = 2 ** 7


def setup_inputs():
    n = np.random.standard_normal
    s = mx_kscale(K)[:, None]
    packed_w1 = pack_fp4(n((K, N)) / np.sqrt(K) / s)
    return {
        "xT": (n((K, T)) * s).astype(np.float32),
        "w1_words": packed_w1[0],
        "w1_scales": packed_w1[1],
        "gate": (np.tile(np.random.uniform(0.2, 1.0, (D, 1, V)) / np.sqrt(D), (1, P, 1))).astype(np.float32),
        "offs": striped(np.random.permutation(T)[:S]),
        "cen": striped(np.random.permutation(S)[:V]),
        "pos1": striped(np.random.permutation(S)[:V]),
        "pos2": striped(np.random.permutation(S)[:V]),
    }


def reference(xT, w1_words, w1_scales, gate, offs, cen, pos1, pos2):
    xq = mxq(f64(xT)[:, unstriped(offs)], 0, "e4m3")
    y = relu(unpack_fp4(w1_words, w1_scales).T @ xq)
    yc = y[:, unstriped(cen)]
    return yc + (y[:, unstriped(pos1)] - yc) * f64(gate)[0, :1] + (y[:, unstriped(pos2)] - yc) * f64(gate)[1, :1]

@@ -1,0 +1,143 @@
+from contextlib import ExitStack
+
+import concourse.mybir as mybir
+
+K, T, S, V, N = 512, 2048, 1024, 512, 256
+P = 128
+FLOPS = 2 * K * S * N
+
+F32 = mybir.dt.float32
+BF16 = mybir.dt.bfloat16
+I32 = mybir.dt.int32
+U32 = mybir.dt.uint32
+U16 = mybir.dt.uint16
+U8 = mybir.dt.uint8
+FP8X4 = mybir.dt.float8_e4m3fn_x4
+FP4X4 = mybir.dt.float4_e2m1fn_x4
+ALU = mybir.AluOpType
+ACT = mybir.ActivationFunctionType
+
+CHUNKS = ((1024, 1024), (1024, 512, 256, 256))
+V_SHARE = ((640, 640), (0, 512, 128, 128))
+PIECES = (512, 256, 256)
+
+
+def tile_picked_grand_relu_e_kernel(
+    tc, xT, w1_words, w1_scales, gate, offs, cen, pos1, pos2, out
+):
+    nc = tc.nc
+    with ExitStack() as ctx:
+        keep = ctx.enter_context(tc.tile_pool(name="keep", bufs=1))
+        psum = ctx.enter_context(tc.psum_pool(name="psum", bufs=1))
+
+        offs_t = keep.tile([P, S // 16], U16, name="offs_t")
+        nc.sync.dma_start(offs_t[:], offs)
+
+        w_scale = keep.tile([P, N], U8, name="w_scale", align_bytes=64)
+        nc.gpsimd.memset(w_scale[:], 0)
+        for q in range(4):
+            nc.gpsimd.dma_start(
+                out=w_scale[32 * q : 32 * q + 4, :].bitcast(I32),
+                in_=w1_scales[0, 4 * q : 4 * q + 4, :].bitcast(I32),
+            )
+
+        x_rows = xT.rearrange("(p j) t -> p j t", j=4)
+        raws = []
+        for u in range(2):
+            c0 = 0
+            for i, w in enumerate(CHUNKS[u]):
+                raw = keep.tile([P, 2, w], F32, name=f"raw{u}_{i}")
+                nc.sync.dma_start(out=raw[:], in_=x_rows[:, 2 * u : 2 * u + 2, c0 : c0 + w])
+                raws.append((u, i, c0, w, raw))
+                c0 = c0 + w
+
+        w_words = keep.tile([P, 2 * N], U8, name="w_words", align_bytes=64)
+        nc.sync.dma_start(out=w_words[:].bitcast(I32), in_=w1_words[0].bitcast(I32))
+        lists = []
+        for name, src in (("cen_t", cen), ("pos1_t", pos1), ("pos2_t", pos2)):
+            lst = keep.tile([P, V // 16], U16, name=name)
+            nc.sync.dma_start(lst[:], src)
+            lists.append(lst)
+        g0 = keep.tile([P, V], F32, name="g0")
+        g1 = keep.tile([P, V], F32, name="g1")
+        nc.sync.dma_start(out=g0[:], in_=gate[0])
+        nc.sync.dma_start(out=g1[:], in_=gate[1])
+
+        pairs = [keep.tile([P, 2 * T], BF16, name=f"pair{u}") for u in range(2)]
+        xq = [keep.tile([P, 4 * n], BF16, name=f"xq{i}", align_bytes=64) for i, n in enumerate(PIECES)]
+
+        def cast(u, i, c0, w, raw):
+            vs = V_SHARE[u][i]
+            dst = pairs[u][:, 2 * c0 : 2 * (c0 + w)].rearrange("p (t e) -> p t e", e=2)
+            src = raw[:].rearrange("p e t -> p t e")
+            if vs > 0:
+                nc.vector.tensor_copy(out=dst[:, 0:vs, :], in_=src[:, 0:vs, :])
+            if vs < w:
+                nc.scalar.copy(out=dst[:, vs:w, :], in_=src[:, vs:w, :])
+
+        def gather(u, i):
+            j0 = sum(PIECES[:i])
+            n = PIECES[i]
+            dst = xq[i][:].bitcast(U32).rearrange("p (c u) -> p c u", u=2)[:, :, u]
+            nc.vector.tensor_copy(
+                out=dst, in_=pairs[u][:].bitcast(U32).indirect(offs_t[:, j0 // 16 : (j0 + n) // 16])
+            )
+
+        y = [keep.tile([P, S], F32, name=f"y{b}") for b in range(2)]
+        accs = {}
+
+        def quant_mm(i):
+            j0 = sum(PIECES[:i])
+            n = PIECES[i]
+            codes = keep.tile([P, n], U32, name=f"codes{i}", align_bytes=64)
+            scales = keep.tile([P, n], U8, name=f"scales{i}", align_bytes=64)
+            nc.vector.quantize_mx(out=codes[:].bitcast(FP8X4), scales=scales[:], in_=xq[i][:])
+            for b in range(2):
+                acc = psum.tile([P, n], F32, name=f"acc{b}_{i}")
+                nc.tensor.matmul_mx(
+                    out=acc[:],
+                    lhsT=w_words[:, 2 * P * b : 2 * P * (b + 1)].bitcast(FP4X4),
+                    lhsT_scale=w_scale[:, P * b : P * (b + 1)],
+                    rhs=codes[:].bitcast(FP8X4),
+                    rhs_scale=scales[:],
+                    start=True,
+                    stop=True,
+                )
+                accs[b, i] = acc
+            nc.scalar.activation(out=y[0][:, j0 : j0 + n], in_=accs[0, i][:], func=ACT.Relu)
+
+        for r in raws:
+            if r[0] == 0:
+                cast(*r)
+        for i in range(len(PIECES)):
+            gather(0, i)
+        for r in raws:
+            if r[0] == 1:
+                cast(*r)
+        gather(1, 0)
+        gather(1, 1)
+        quant_mm(0)
+        gather(1, 2)
+        quant_mm(1)
+        quant_mm(2)
+
+        one_minus = keep.tile([P, V], F32, name="one_minus")
+        nc.vector.tensor_scalar(out=one_minus[:], in0=g0[:], scalar1=-1.0, scalar2=1.0, op0=ALU.mult, op1=ALU.add)
+        gc = keep.tile([P, V], F32, name="gc")
+        nc.vector.tensor_tensor(out=gc[:], in0=one_minus[:], in1=g1[:], op=ALU.subtract)
+        for i in range(len(PIECES)):
+            j0 = sum(PIECES[:i])
+            nc.scalar.activation(out=y[1][:, j0 : j0 + PIECES[i]], in_=accs[1, i][:], func=ACT.Relu)
+
+        for b in range(2):
+            terms = []
+            for d, (lst, g) in enumerate(zip(lists, (gc, g0, g1))):
+                if d == 2:
+                    part = keep.tile([P, V], F32, name=f"part{b}")
+                    nc.vector.tensor_tensor(out=part[:], in0=terms[0][:], in1=terms[1][:], op=ALU.add)
+                term = keep.tile([P, V], F32, name=f"term{b}_{d}")
+                nc.vector.tensor_tensor(out=term[:], in0=y[b][:].indirect(lst[:]), in1=g[:], op=ALU.mult)
+                terms.append(term)
+            res = keep.tile([P, V], F32, name=f"res{b}")
+            nc.vector.tensor_tensor(out=res[:], in0=part[:], in1=terms[2][:], op=ALU.add)
+            nc.sync.dma_start(out=out[P * b : P * (b + 1), :], in_=res[:])

@@ -1,6 +1,7 @@
 from contextlib import ExitStack
 
 import concourse.mybir as mybir
+from concourse.masks import make_identity
 
 K, T, S, V, N = 512, 2048, 1024, 512, 256
 P = 128
@@ -17,9 +18,11 @@ FP4X4 = mybir.dt.float4_e2m1fn_x4
 ALU = mybir.AluOpType
 ACT = mybir.ActivationFunctionType
 
-CHUNKS = ((1024, 1024), (1024, 512, 256, 256))
-V_SHARE = ((640, 640), (0, 512, 128, 128))
-PIECES = (512, 256, 256)
+CHUNKS = ((1024, 1024), (512, 512, 512, 256, 256))
+V_SHARE = ((640, 640), (0, 0, 320, 160, 160))
+PIECE = 256
+PIECES = S // PIECE
+VCH = V // P
 
 
 def tile_picked_grand_relu_e_kernel(
@@ -30,19 +33,9 @@ def tile_picked_grand_relu_e_kernel(
         keep = ctx.enter_context(tc.tile_pool(name="keep", bufs=1))
         psum = ctx.enter_context(tc.psum_pool(name="psum", bufs=1))
 
-        offs_t = keep.tile([P, S // 16], U16, name="offs_t")
-        nc.sync.dma_start(offs_t[:], offs)
-
-        w_scale = keep.tile([P, N], U8, name="w_scale", align_bytes=64)
-        nc.gpsimd.memset(w_scale[:], 0)
-        for q in range(4):
-            nc.gpsimd.dma_start(
-                out=w_scale[32 * q : 32 * q + 4, :].bitcast(I32),
-                in_=w1_scales[0, 4 * q : 4 * q + 4, :].bitcast(I32),
-            )
-
         x_rows = xT.rearrange("(p j) t -> p j t", j=4)
         raws = []
+        offs_t = keep.tile([P, S // 16], U16, name="offs_t")
         for u in range(2):
             c0 = 0
             for i, w in enumerate(CHUNKS[u]):
@@ -50,6 +43,8 @@ def tile_picked_grand_relu_e_kernel(
                 nc.sync.dma_start(out=raw[:], in_=x_rows[:, 2 * u : 2 * u + 2, c0 : c0 + w])
                 raws.append((u, i, c0, w, raw))
                 c0 = c0 + w
+            if u == 0:
+                nc.sync.dma_start(offs_t[:], offs)
 
         w_words = keep.tile([P, 2 * N], U8, name="w_words", align_bytes=64)
         nc.sync.dma_start(out=w_words[:].bitcast(I32), in_=w1_words[0].bitcast(I32))
@@ -58,13 +53,31 @@ def tile_picked_grand_relu_e_kernel(
             lst = keep.tile([P, V // 16], U16, name=name)
             nc.sync.dma_start(lst[:], src)
             lists.append(lst)
-        g0 = keep.tile([P, V], F32, name="g0")
         g1 = keep.tile([P, V], F32, name="g1")
-        nc.sync.dma_start(out=g0[:], in_=gate[0])
         nc.sync.dma_start(out=g1[:], in_=gate[1])
 
+        g_cols = [keep.tile([P, VCH], F32, name=f"g_col{d}") for d in range(2)]
+        with nc.allow_non_contiguous_dma(reason="one gate value a partition"):
+            for d in range(2):
+                nc.sync.dma_start(out=g_cols[d][:], in_=gate[d, 0, :].rearrange("(c v) -> v c", v=P))
+        w_scale = keep.tile([P, N], U8, name="w_scale", align_bytes=64)
+        nc.gpsimd.memset(w_scale[:], 0)
+        for q in range(4):
+            nc.gpsimd.dma_start(
+                out=w_scale[32 * q : 32 * q + 4, :].bitcast(I32),
+                in_=w1_scales[0, 4 * q : 4 * q + 4, :].bitcast(I32),
+            )
+        ident = keep.tile([P, P], F32, name="ident")
+        make_identity(nc, ident[:])
+
+        g_sum = keep.tile([P, VCH], F32, name="g_sum")
+        nc.gpsimd.tensor_tensor(out=g_sum[:], in0=g_cols[0][:], in1=g_cols[1][:], op=ALU.add)
+        gc_col = keep.tile([P, VCH], F32, name="gc_col")
+        nc.gpsimd.tensor_scalar(out=gc_col[:], in0=g_sum[:], scalar1=-1.0, scalar2=1.0, op0=ALU.mult, op1=ALU.add)
+
         pairs = [keep.tile([P, 2 * T], BF16, name=f"pair{u}") for u in range(2)]
-        xq = [keep.tile([P, 4 * n], BF16, name=f"xq{i}", align_bytes=64) for i, n in enumerate(PIECES)]
+        picked = [keep.tile([P, 2, PIECE], U32, name=f"picked{i}") for i in range(PIECES)]
+        xq = [keep.tile([P, 2 * PIECE], U32, name=f"xq{i}", align_bytes=64) for i in range(PIECES)]
 
         def cast(u, i, c0, w, raw):
             vs = V_SHARE[u][i]
@@ -76,68 +89,92 @@ def tile_picked_grand_relu_e_kernel(
                 nc.scalar.copy(out=dst[:, vs:w, :], in_=src[:, vs:w, :])
 
         def gather(u, i):
-            j0 = sum(PIECES[:i])
-            n = PIECES[i]
-            dst = xq[i][:].bitcast(U32).rearrange("p (c u) -> p c u", u=2)[:, :, u]
             nc.vector.tensor_copy(
-                out=dst, in_=pairs[u][:].bitcast(U32).indirect(offs_t[:, j0 // 16 : (j0 + n) // 16])
+                out=picked[i][:, u, :],
+                in_=pairs[u][:].bitcast(U32).indirect(offs_t[:, i * PIECE // 16 : (i + 1) * PIECE // 16]),
             )
 
         y = [keep.tile([P, S], F32, name=f"y{b}") for b in range(2)]
-        accs = {}
+        codes = keep.tile([P, S], U32, name="codes", align_bytes=64)
+        scales = keep.tile([P, S], U8, name="scales", align_bytes=64)
 
-        def quant_mm(i):
-            j0 = sum(PIECES[:i])
-            n = PIECES[i]
-            codes = keep.tile([P, n], U32, name=f"codes{i}", align_bytes=64)
-            scales = keep.tile([P, n], U8, name=f"scales{i}", align_bytes=64)
-            nc.vector.quantize_mx(out=codes[:].bitcast(FP8X4), scales=scales[:], in_=xq[i][:])
-            for b in range(2):
-                acc = psum.tile([P, n], F32, name=f"acc{b}_{i}")
-                nc.tensor.matmul_mx(
-                    out=acc[:],
-                    lhsT=w_words[:, 2 * P * b : 2 * P * (b + 1)].bitcast(FP4X4),
-                    lhsT_scale=w_scale[:, P * b : P * (b + 1)],
-                    rhs=codes[:].bitcast(FP8X4),
-                    rhs_scale=scales[:],
-                    start=True,
-                    stop=True,
-                )
-                accs[b, i] = acc
-            nc.scalar.activation(out=y[0][:, j0 : j0 + n], in_=accs[0, i][:], func=ACT.Relu)
+        def product(b, j0, n, bank, on_vector):
+            acc = psum.tile([P, n], F32, name=f"acc{b}_{j0}", tag=bank)
+            nc.tensor.matmul_mx(
+                out=acc[:],
+                lhsT=w_words[:, 2 * P * b : 2 * P * (b + 1)].bitcast(FP4X4),
+                lhsT_scale=w_scale[:, P * b : P * (b + 1)],
+                rhs=codes[:, j0 : j0 + n].bitcast(FP8X4),
+                rhs_scale=scales[:, j0 : j0 + n],
+                start=True,
+                stop=True,
+            )
+            if on_vector:
+                nc.vector.tensor_scalar_max(out=y[b][:, j0 : j0 + n], in0=acc[:], scalar1=0.0)
+            else:
+                nc.scalar.activation(out=y[b][:, j0 : j0 + n], in_=acc[:], func=ACT.Relu)
 
         for r in raws:
             if r[0] == 0:
                 cast(*r)
-        for i in range(len(PIECES)):
+        for i in range(PIECES):
             gather(0, i)
         for r in raws:
             if r[0] == 1:
                 cast(*r)
-        gather(1, 0)
-        gather(1, 1)
-        quant_mm(0)
-        gather(1, 2)
-        quant_mm(1)
-        quant_mm(2)
+        for i in range(PIECES):
+            gather(1, i)
+            nc.scalar.copy(
+                out=xq[i][:].rearrange("p (c u) -> p c u", u=2), in_=picked[i][:].rearrange("p u c -> p c u")
+            )
+        j0 = 0
+        for i, n in enumerate((256, 256, 256, 128, 128)):
+            cols = slice(j0, j0 + n)
+            piece, first = divmod(j0, PIECE)
+            nc.vector.quantize_mx(
+                out=codes[:, cols].bitcast(FP8X4),
+                scales=scales[:, cols],
+                in_=xq[piece][:, 2 * first : 2 * (first + n)].bitcast(BF16),
+            )
+            product(0, j0, n, f"mm{i}", i >= 3)
+            j0 = j0 + n
+        for h in range(2):
+            product(1, h * 512, 512, f"mm{3 + h}", False)
 
-        one_minus = keep.tile([P, V], F32, name="one_minus")
-        nc.vector.tensor_scalar(out=one_minus[:], in0=g0[:], scalar1=-1.0, scalar2=1.0, op0=ALU.mult, op1=ALU.add)
-        gc = keep.tile([P, V], F32, name="gc")
-        nc.vector.tensor_tensor(out=gc[:], in0=one_minus[:], in1=g1[:], op=ALU.subtract)
-        for i in range(len(PIECES)):
-            j0 = sum(PIECES[:i])
-            nc.scalar.activation(out=y[1][:, j0 : j0 + PIECES[i]], in_=accs[1, i][:], func=ACT.Relu)
-
+        banks = ("fw0", "mm0", "mm1", "mm2")
+        sums = []
         for b in range(2):
-            terms = []
-            for d, (lst, g) in enumerate(zip(lists, (gc, g0, g1))):
-                if d == 2:
-                    part = keep.tile([P, V], F32, name=f"part{b}")
-                    nc.vector.tensor_tensor(out=part[:], in0=terms[0][:], in1=terms[1][:], op=ALU.add)
-                term = keep.tile([P, V], F32, name=f"term{b}_{d}")
-                nc.vector.tensor_tensor(out=term[:], in0=y[b][:].indirect(lst[:]), in1=g[:], op=ALU.mult)
-                terms.append(term)
-            res = keep.tile([P, V], F32, name=f"res{b}")
-            nc.vector.tensor_tensor(out=res[:], in0=part[:], in1=terms[2][:], op=ALU.add)
-            nc.sync.dma_start(out=out[P * b : P * (b + 1), :], in_=res[:])
+            acc = psum.tile([P, V], F32, name=f"sum{b}")
+            sums.append(acc)
+            for d, g_col in enumerate((gc_col, g_cols[0])):
+                got = keep.tile([P, V], F32, name=f"got{b}_{d}", tag=f"got{b}_{d}")
+                nc.vector.tensor_copy(out=got[:], in_=y[b][:].indirect(lists[d][:]))
+                turned = psum.tile([P, V], F32, name=f"turned{b}_{d}", tag=banks[2 * b + d])
+                for c in range(VCH):
+                    cols = slice(c * P, (c + 1) * P)
+                    nc.tensor.transpose(turned[:, cols], got[:, cols], ident[:])
+                scaled = keep.tile([P, V], F32, name=f"scaled{b}_{d}")
+                for c in range(VCH):
+                    cols = slice(c * P, (c + 1) * P)
+                    nc.scalar.activation(
+                        out=scaled[:, cols], in_=turned[:, cols], func=ACT.Copy, scale=g_col[:, c : c + 1]
+                    )
+                for c in range(VCH):
+                    cols = slice(c * P, (c + 1) * P)
+                    nc.tensor.matmul(
+                        acc[:, cols],
+                        scaled[:, cols],
+                        ident[:],
+                        start=(d == 0 and c == 0),
+                        stop=(d == 1 and c == VCH - 1),
+                        is_transpose=True,
+                    )
+        terms = []
+        for b in range(2):
+            term = keep.tile([P, V], F32, name=f"term{b}", tag=("got1_0", "term1")[b])
+            nc.vector.tensor_tensor(out=term[:], in0=y[b][:].indirect(lists[2][:]), in1=g1[:], op=ALU.mult)
+            terms.append(term)
+        for b, v0, v1 in ((0, 0, V), (1, 0, V // 2), (1, V // 2, V)):
+            res = keep.tile([P, v1 - v0], F32, name=f"res{b}_{v0}")
+            nc.vector.tensor_tensor(out=res[:], in0=terms[b][:, v0:v1], in1=sums[b][:, v0:v1], op=ALU.add)
+            nc.sync.dma_start(out=out[P * b : P * (b + 1), v0:v1], in_=res[:])

@@ -33,6 +33,13 @@ def tile_picked_grand_relu_e_kernel(
         keep = ctx.enter_context(tc.tile_pool(name="keep", bufs=1))
         psum = ctx.enter_context(tc.psum_pool(name="psum", bufs=1))
 
+        g_rows = keep.tile([P, P], F32, name="g_rows")
+        nc.gpsimd.memset(g_rows[:], 0.0)
+        gate_chunks = gate.rearrange("d p (c v) -> (d p c) v", v=P)
+        nc.sync.dma_start(out=g_rows[0 : 2 * VCH, :], in_=gate_chunks[0 :: 32 * VCH + 1, :])
+        ident = keep.tile([P, P], F32, name="ident")
+        make_identity(nc, ident[:])
+
         x_rows = xT.rearrange("(p j) t -> p j t", j=4)
         raws = []
         offs_t = keep.tile([P, S // 16], U16, name="offs_t")
@@ -48,32 +55,42 @@ def tile_picked_grand_relu_e_kernel(
 
         w_words = keep.tile([P, 2 * N], U8, name="w_words", align_bytes=64)
         nc.sync.dma_start(out=w_words[:].bitcast(I32), in_=w1_words[0].bitcast(I32))
+        w_scale = keep.tile([P, N], U8, name="w_scale", align_bytes=64)
+        nc.gpsimd.memset(w_scale[:], 0)
+        for q in range(4):
+            nc.sync.dma_start(
+                out=w_scale[32 * q : 32 * q + 4, :].bitcast(I32),
+                in_=w1_scales[0, 4 * q : 4 * q + 4, :].bitcast(I32),
+            )
         lists = []
         for name, src in (("cen_t", cen), ("pos1_t", pos1), ("pos2_t", pos2)):
             lst = keep.tile([P, V // 16], U16, name=name)
             nc.sync.dma_start(lst[:], src)
             lists.append(lst)
-        g1 = keep.tile([P, V], F32, name="g1")
-        nc.sync.dma_start(out=g1[:], in_=gate[1])
-
-        g_cols = [keep.tile([P, VCH], F32, name=f"g_col{d}") for d in range(2)]
-        with nc.allow_non_contiguous_dma(reason="one gate value a partition"):
-            for d in range(2):
-                nc.sync.dma_start(out=g_cols[d][:], in_=gate[d, 0, :].rearrange("(c v) -> v c", v=P))
-        w_scale = keep.tile([P, N], U8, name="w_scale", align_bytes=64)
-        nc.gpsimd.memset(w_scale[:], 0)
-        for q in range(4):
-            nc.gpsimd.dma_start(
-                out=w_scale[32 * q : 32 * q + 4, :].bitcast(I32),
-                in_=w1_scales[0, 4 * q : 4 * q + 4, :].bitcast(I32),
-            )
-        ident = keep.tile([P, P], F32, name="ident")
-        make_identity(nc, ident[:])
-
-        g_sum = keep.tile([P, VCH], F32, name="g_sum")
-        nc.gpsimd.tensor_tensor(out=g_sum[:], in0=g_cols[0][:], in1=g_cols[1][:], op=ALU.add)
-        gc_col = keep.tile([P, VCH], F32, name="gc_col")
-        nc.gpsimd.tensor_scalar(out=gc_col[:], in0=g_sum[:], scalar1=-1.0, scalar2=1.0, op0=ALU.mult, op1=ALU.add)
+        gates = []
+        for d in range(2):
+            g = keep.tile([P, V], F32, name=f"g{d}")
+            nc.sync.dma_start(out=g[:], in_=gate[d])
+            gates.append(g)
+        g_turned = psum.tile([P, P], F32, name="g_turned", tag="bk0")
+        nc.tensor.transpose(g_turned[:], g_rows[:], ident[:])
+        g_cols = keep.tile([P, 2 * VCH], F32, name="g_cols")
+        nc.scalar.copy(out=g_cols[:], in_=g_turned[:, 0 : 2 * VCH])
+        g_sum = psum.tile([P, V], F32, name="g_sum", tag="bk1")
+        for d in range(2):
+            for c in range(VCH):
+                col = VCH * d + c
+                nc.tensor.matmul(
+                    g_sum[:, c * P : (c + 1) * P],
+                    g_cols[:, col : col + 1].to_broadcast([P, P]),
+                    ident[:],
+                    start=(d == 0 and c == 0),
+                    stop=(d == 1 and c == VCH - 1),
+                    is_transpose=True,
+                )
+        gc = keep.tile([P, V], F32, name="gc")
+        nc.scalar.activation(out=gc[:], in_=g_sum[:], func=ACT.Copy, scale=-1.0, bias=1.0)
+        factors = (gc, gates[0], gates[1])
 
         pairs = [keep.tile([P, 2 * T], BF16, name=f"pair{u}") for u in range(2)]
         picked = [keep.tile([P, 2, PIECE], U32, name=f"picked{i}") for i in range(PIECES)]
@@ -141,40 +158,46 @@ def tile_picked_grand_relu_e_kernel(
         for h in range(2):
             product(1, h * 512, 512, f"mm{3 + h}", False)
 
-        banks = ("fw0", "mm0", "mm1", "mm2")
-        sums = []
-        for b in range(2):
-            acc = psum.tile([P, V], F32, name=f"sum{b}")
-            sums.append(acc)
-            for d, g_col in enumerate((gc_col, g_cols[0])):
-                got = keep.tile([P, V], F32, name=f"got{b}_{d}", tag=f"got{b}_{d}")
-                nc.vector.tensor_copy(out=got[:], in_=y[b][:].indirect(lists[d][:]))
-                turned = psum.tile([P, V], F32, name=f"turned{b}_{d}", tag=banks[2 * b + d])
-                for c in range(VCH):
-                    cols = slice(c * P, (c + 1) * P)
-                    nc.tensor.transpose(turned[:, cols], got[:, cols], ident[:])
-                scaled = keep.tile([P, V], F32, name=f"scaled{b}_{d}")
-                for c in range(VCH):
-                    cols = slice(c * P, (c + 1) * P)
-                    nc.scalar.activation(
-                        out=scaled[:, cols], in_=turned[:, cols], func=ACT.Copy, scale=g_col[:, c : c + 1]
-                    )
-                for c in range(VCH):
+        def term(b, d, v0, v1):
+            got = keep.tile([P, v1 - v0], F32, name=f"got{b}_{d}_{v0}")
+            nc.vector.tensor_tensor(
+                out=got[:],
+                in0=y[b][:].indirect(lists[d][:, v0 // 16 : v1 // 16]),
+                in1=factors[d][:, v0:v1],
+                op=ALU.mult,
+            )
+            return got
+
+        def sum_by_transposes(b, v0, v1, fw_bank, bk_bank):
+            n = v1 - v0
+            turned = psum.tile([P, n], F32, name=f"turned{b}", tag=fw_bank)
+            for d in range(3):
+                got = term(b, d, v0, v1)
+                for c in range(n // P):
                     cols = slice(c * P, (c + 1) * P)
                     nc.tensor.matmul(
-                        acc[:, cols],
-                        scaled[:, cols],
+                        turned[:, cols],
+                        got[:, cols],
                         ident[:],
                         start=(d == 0 and c == 0),
-                        stop=(d == 1 and c == VCH - 1),
+                        stop=(d == 2 and c == n // P - 1),
                         is_transpose=True,
                     )
-        terms = []
-        for b in range(2):
-            term = keep.tile([P, V], F32, name=f"term{b}", tag=("got1_0", "term1")[b])
-            nc.vector.tensor_tensor(out=term[:], in0=y[b][:].indirect(lists[2][:]), in1=g1[:], op=ALU.mult)
-            terms.append(term)
-        for b, v0, v1 in ((0, 0, V), (1, 0, V // 2), (1, V // 2, V)):
-            res = keep.tile([P, v1 - v0], F32, name=f"res{b}_{v0}")
-            nc.vector.tensor_tensor(out=res[:], in0=terms[b][:, v0:v1], in1=sums[b][:, v0:v1], op=ALU.add)
-            nc.sync.dma_start(out=out[P * b : P * (b + 1), v0:v1], in_=res[:])
+            summed = keep.tile([P, n], F32, name=f"summed{b}")
+            nc.scalar.copy(out=summed[:], in_=turned[:])
+            back = psum.tile([P, n], F32, name=f"back{b}", tag=bk_bank)
+            for c in range(n // P):
+                cols = slice(c * P, (c + 1) * P)
+                nc.tensor.transpose(back[:, cols], summed[:, cols], ident[:])
+            res = keep.tile([P, n], F32, name=f"res{b}")
+            nc.scalar.copy(out=res[:], in_=back[:])
+            nc.scalar.dma_start(out=out[P * b : P * (b + 1), v0:v1], in_=res[:])
+
+        sum_by_transposes(0, 0, V, "fw0", "bk0")
+        sum_by_transposes(1, 0, V // 2, "mm0", "bk1")
+        last = [term(1, d, V // 2, V) for d in range(3)]
+        part = keep.tile([P, V // 2], F32, name="part")
+        nc.vector.tensor_tensor(out=part[:], in0=last[0][:], in1=last[1][:], op=ALU.add)
+        res = keep.tile([P, V // 2], F32, name="res_last")
+        nc.vector.tensor_tensor(out=res[:], in0=part[:], in1=last[2][:], op=ALU.add)
+        nc.sync.dma_start(out=out[P : 2 * P, V // 2 : V], in_=res[:])

@@ -18,8 +18,9 @@ FP4X4 = mybir.dt.float4_e2m1fn_x4
 ALU = mybir.AluOpType
 ACT = mybir.ActivationFunctionType
 
-CHUNKS = ((1024, 1024), (512, 512, 512, 256, 256))
-V_SHARE = ((640, 640), (0, 0, 320, 160, 160))
+PAIR_CHUNKS = (1024, 768, 256)
+V_SHARE = (384, 512, 160)
+LAST_CHUNKS = (512, 512, 512, 512)
 PIECE = 256
 PIECES = S // PIECE
 VCH = V // P
@@ -41,17 +42,22 @@ def tile_picked_grand_relu_e_kernel(
         make_identity(nc, ident[:])
 
         x_rows = xT.rearrange("(p j) t -> p j t", j=4)
-        raws = []
+        raw2 = keep.tile([P, T], F32, name="raw2", tag="single")
+        nc.sync.dma_start(out=raw2[:], in_=x_rows[:, 2, :])
         offs_t = keep.tile([P, S // 16], U16, name="offs_t")
-        for u in range(2):
-            c0 = 0
-            for i, w in enumerate(CHUNKS[u]):
-                raw = keep.tile([P, 2, w], F32, name=f"raw{u}_{i}")
-                nc.sync.dma_start(out=raw[:], in_=x_rows[:, 2 * u : 2 * u + 2, c0 : c0 + w])
-                raws.append((u, i, c0, w, raw))
-                c0 = c0 + w
-            if u == 0:
-                nc.sync.dma_start(offs_t[:], offs)
+        nc.sync.dma_start(offs_t[:], offs)
+        raws = []
+        c0 = 0
+        for i, w in enumerate(PAIR_CHUNKS):
+            raw = keep.tile([P, 2, w], F32, name=f"raw01_{i}")
+            nc.sync.dma_start(out=raw[:], in_=x_rows[:, 0:2, c0 : c0 + w])
+            raws.append((i, c0, w, raw))
+            c0 = c0 + w
+        raw3 = keep.tile([P, T], F32, name="raw3")
+        c0 = 0
+        for w in LAST_CHUNKS:
+            nc.sync.dma_start(out=raw3[:, c0 : c0 + w], in_=x_rows[:, 3, c0 : c0 + w])
+            c0 = c0 + w
 
         w_words = keep.tile([P, 2 * N], U8, name="w_words", align_bytes=64)
         nc.sync.dma_start(out=w_words[:].bitcast(I32), in_=w1_words[0].bitcast(I32))
@@ -92,24 +98,15 @@ def tile_picked_grand_relu_e_kernel(
         nc.scalar.activation(out=gc[:], in_=g_sum[:], func=ACT.Copy, scale=-1.0, bias=1.0)
         factors = (gc, gates[0], gates[1])
 
-        pairs = [keep.tile([P, 2 * T], BF16, name=f"pair{u}") for u in range(2)]
-        picked = [keep.tile([P, 2, PIECE], U32, name=f"picked{i}") for i in range(PIECES)]
-        xq = [keep.tile([P, 2 * PIECE], U32, name=f"xq{i}", align_bytes=64) for i in range(PIECES)]
+        pair = keep.tile([P, 2 * T], BF16, name="pair")
+        plane3 = keep.tile([P, T], BF16, name="plane3", tag="single")
+        xq = [keep.tile([P, 4 * PIECE], BF16, name=f"xq{i}", align_bytes=64) for i in range(PIECES)]
 
-        def cast(u, i, c0, w, raw):
-            vs = V_SHARE[u][i]
-            dst = pairs[u][:, 2 * c0 : 2 * (c0 + w)].rearrange("p (t e) -> p t e", e=2)
-            src = raw[:].rearrange("p e t -> p t e")
-            if vs > 0:
-                nc.vector.tensor_copy(out=dst[:, 0:vs, :], in_=src[:, 0:vs, :])
-            if vs < w:
-                nc.scalar.copy(out=dst[:, vs:w, :], in_=src[:, vs:w, :])
+        def entries(i):
+            return offs_t[:, i * PIECE // 16 : (i + 1) * PIECE // 16]
 
-        def gather(u, i):
-            nc.vector.tensor_copy(
-                out=picked[i][:, u, :],
-                in_=pairs[u][:].bitcast(U32).indirect(offs_t[:, i * PIECE // 16 : (i + 1) * PIECE // 16]),
-            )
+        def slot(i, t):
+            return xq[i][:].rearrange("p (c t) -> p c t", t=4)[:, :, t]
 
         y = [keep.tile([P, S], F32, name=f"y{b}") for b in range(2)]
         codes = keep.tile([P, S], U32, name="codes", align_bytes=64)
@@ -131,30 +128,35 @@ def tile_picked_grand_relu_e_kernel(
             else:
                 nc.scalar.activation(out=y[b][:, j0 : j0 + n], in_=acc[:], func=ACT.Relu)
 
-        for r in raws:
-            if r[0] == 0:
-                cast(*r)
         for i in range(PIECES):
-            gather(0, i)
-        for r in raws:
-            if r[0] == 1:
-                cast(*r)
+            nc.vector.tensor_copy(out=slot(i, 2), in_=raw2[:].indirect(entries(i)))
+        for i, c0, w, raw in raws:
+            vs = V_SHARE[i]
+            dst = pair[:, 2 * c0 : 2 * (c0 + w)].rearrange("p (t e) -> p t e", e=2)
+            src = raw[:].rearrange("p e t -> p t e")
+            nc.scalar.copy(out=dst[:, vs:w, :], in_=src[:, vs:w, :])
+            nc.vector.tensor_copy(out=dst[:, 0:vs, :], in_=src[:, 0:vs, :])
         for i in range(PIECES):
-            gather(1, i)
-            nc.scalar.copy(
-                out=xq[i][:].rearrange("p (c u) -> p c u", u=2), in_=picked[i][:].rearrange("p u c -> p c u")
+            nc.vector.tensor_copy(
+                out=xq[i][:].bitcast(U32).rearrange("p (c u) -> p c u", u=2)[:, :, 0],
+                in_=pair[:].bitcast(U32).indirect(entries(i)),
             )
-        j0 = 0
-        for i, n in enumerate((256, 256, 256, 128, 128)):
+        c0 = 0
+        for w in LAST_CHUNKS:
+            nc.scalar.copy(out=plane3[:, c0 : c0 + w], in_=raw3[:, c0 : c0 + w])
+            c0 = c0 + w
+        for i in range(PIECES - 1):
+            nc.scalar.activation(out=slot(i, 3), in_=plane3[:].indirect(entries(i)), func=ACT.Copy)
+        nc.vector.tensor_copy(out=slot(PIECES - 1, 3), in_=raw3[:].indirect(entries(PIECES - 1)))
+        for piece, first, n, on_vector in ((0, 0, 256, False), (1, 0, 256, False), (3, 0, 256, False), (2, 0, 128, True), (2, 128, 128, True)):
+            j0 = piece * PIECE + first
             cols = slice(j0, j0 + n)
-            piece, first = divmod(j0, PIECE)
             nc.vector.quantize_mx(
                 out=codes[:, cols].bitcast(FP8X4),
                 scales=scales[:, cols],
-                in_=xq[piece][:, 2 * first : 2 * (first + n)].bitcast(BF16),
+                in_=xq[piece][:, 4 * first : 4 * (first + n)],
             )
-            product(0, j0, n, f"mm{i}", i >= 3)
-            j0 = j0 + n
+            product(0, j0, n, f"mm{(piece, 4)[first > 0]}", on_vector)
         for h in range(2):
             product(1, h * 512, 512, f"mm{3 + h}", False)
 

@@ -19,8 +19,8 @@ ALU = mybir.AluOpType
 ACT = mybir.ActivationFunctionType
 
 PAIR_CHUNKS = (1024, 768, 256)
-V_SHARE = (384, 512, 160)
-LAST_CHUNKS = (512, 512, 512, 512)
+V_SHARE = (224, 512, 160)
+LAST_CHUNKS = (640, 544, 480, 384)
 PIECE = 256
 PIECES = S // PIECE
 VCH = V // P
@@ -35,21 +35,21 @@ def tile_picked_grand_relu_e_kernel(
         psum = ctx.enter_context(tc.psum_pool(name="psum", bufs=1))
 
         g_rows = keep.tile([P, P], F32, name="g_rows")
-        nc.gpsimd.memset(g_rows[:], 0.0)
+        nc.gpsimd.memset(g_rows[0 : P - 2 * VCH, :], 0.0)
         gate_chunks = gate.rearrange("d p (c v) -> (d p c) v", v=P)
-        nc.sync.dma_start(out=g_rows[0 : 2 * VCH, :], in_=gate_chunks[0 :: 32 * VCH + 1, :])
+        nc.scalar.dma_start(out=g_rows[P - 2 * VCH : P, :], in_=gate_chunks[0 :: 32 * VCH + 1, :])
         ident = keep.tile([P, P], F32, name="ident")
         make_identity(nc, ident[:])
 
         x_rows = xT.rearrange("(p j) t -> p j t", j=4)
-        raw2 = keep.tile([P, T], F32, name="raw2", tag="single")
+        raw2 = keep.tile([P, T], F32, name="raw2")
         nc.sync.dma_start(out=raw2[:], in_=x_rows[:, 2, :])
         offs_t = keep.tile([P, S // 16], U16, name="offs_t")
         nc.sync.dma_start(offs_t[:], offs)
         raws = []
         c0 = 0
         for i, w in enumerate(PAIR_CHUNKS):
-            raw = keep.tile([P, 2, w], F32, name=f"raw01_{i}")
+            raw = keep.tile([P, 2, w], F32, name=f"raw01_{i}", tag=("raw0", "raw1", "single")[i])
             nc.sync.dma_start(out=raw[:], in_=x_rows[:, 0:2, c0 : c0 + w])
             raws.append((i, c0, w, raw))
             c0 = c0 + w
@@ -68,20 +68,17 @@ def tile_picked_grand_relu_e_kernel(
                 out=w_scale[32 * q : 32 * q + 4, :].bitcast(I32),
                 in_=w1_scales[0, 4 * q : 4 * q + 4, :].bitcast(I32),
             )
+        gates = keep.tile([P, 2, V], F32, name="gates")
+        nc.sync.dma_start(out=gates[:], in_=gate.rearrange("d p v -> p d v"))
         lists = []
-        for name, src in (("cen_t", cen), ("pos1_t", pos1), ("pos2_t", pos2)):
+        for name, src in (("pos1_t", pos1), ("pos2_t", pos2), ("cen_t", cen)):
             lst = keep.tile([P, V // 16], U16, name=name)
             nc.sync.dma_start(lst[:], src)
             lists.append(lst)
-        gates = []
-        for d in range(2):
-            g = keep.tile([P, V], F32, name=f"g{d}")
-            nc.sync.dma_start(out=g[:], in_=gate[d])
-            gates.append(g)
         g_turned = psum.tile([P, P], F32, name="g_turned", tag="bk0")
         nc.tensor.transpose(g_turned[:], g_rows[:], ident[:])
         g_cols = keep.tile([P, 2 * VCH], F32, name="g_cols")
-        nc.scalar.copy(out=g_cols[:], in_=g_turned[:, 0 : 2 * VCH])
+        nc.scalar.copy(out=g_cols[:], in_=g_turned[:, P - 2 * VCH : P])
         g_sum = psum.tile([P, V], F32, name="g_sum", tag="bk1")
         for d in range(2):
             for c in range(VCH):
@@ -94,25 +91,24 @@ def tile_picked_grand_relu_e_kernel(
                     stop=(d == 1 and c == VCH - 1),
                     is_transpose=True,
                 )
-        gc = keep.tile([P, V], F32, name="gc")
-        nc.scalar.activation(out=gc[:], in_=g_sum[:], func=ACT.Copy, scale=-1.0, bias=1.0)
-        factors = (gc, gates[0], gates[1])
 
         pair = keep.tile([P, 2 * T], BF16, name="pair")
         plane3 = keep.tile([P, T], BF16, name="plane3", tag="single")
-        xq = [keep.tile([P, 4 * PIECE], BF16, name=f"xq{i}", align_bytes=64) for i in range(PIECES)]
+        xq = keep.tile([P, 4 * S], BF16, name="xq", align_bytes=64)
+        xq_slots = xq[:].rearrange("p (c t) -> p c t", t=4)
+        xq_words = xq[:].bitcast(U32).rearrange("p (c u) -> p c u", u=2)
 
         def entries(i):
             return offs_t[:, i * PIECE // 16 : (i + 1) * PIECE // 16]
 
         def slot(i, t):
-            return xq[i][:].rearrange("p (c t) -> p c t", t=4)[:, :, t]
+            return xq_slots[:, i * PIECE : (i + 1) * PIECE, t]
 
-        y = [keep.tile([P, S], F32, name=f"y{b}") for b in range(2)]
+        y = [keep.tile([P, S], F32, name=f"y{b}", tag=("single", "y1")[b]) for b in range(2)]
         codes = keep.tile([P, S], U32, name="codes", align_bytes=64)
         scales = keep.tile([P, S], U8, name="scales", align_bytes=64)
 
-        def product(b, j0, n, bank, on_vector):
+        def product(b, j0, n, bank):
             acc = psum.tile([P, n], F32, name=f"acc{b}_{j0}", tag=bank)
             nc.tensor.matmul_mx(
                 out=acc[:],
@@ -123,13 +119,15 @@ def tile_picked_grand_relu_e_kernel(
                 start=True,
                 stop=True,
             )
+            return acc
+
+        def relu(b, j0, n, acc, on_vector):
             if on_vector:
                 nc.vector.tensor_scalar_max(out=y[b][:, j0 : j0 + n], in0=acc[:], scalar1=0.0)
             else:
                 nc.scalar.activation(out=y[b][:, j0 : j0 + n], in_=acc[:], func=ACT.Relu)
 
-        for i in range(PIECES):
-            nc.vector.tensor_copy(out=slot(i, 2), in_=raw2[:].indirect(entries(i)))
+        nc.vector.tensor_copy(out=xq_slots[:, :, 2], in_=raw2[:].indirect(offs_t[:]))
         for i, c0, w, raw in raws:
             vs = V_SHARE[i]
             dst = pair[:, 2 * c0 : 2 * (c0 + w)].rearrange("p (t e) -> p t e", e=2)
@@ -138,7 +136,7 @@ def tile_picked_grand_relu_e_kernel(
             nc.vector.tensor_copy(out=dst[:, 0:vs, :], in_=src[:, 0:vs, :])
         for i in range(PIECES):
             nc.vector.tensor_copy(
-                out=xq[i][:].bitcast(U32).rearrange("p (c u) -> p c u", u=2)[:, :, 0],
+                out=xq_words[:, i * PIECE : (i + 1) * PIECE, 0],
                 in_=pair[:].bitcast(U32).indirect(entries(i)),
             )
         c0 = 0
@@ -154,11 +152,16 @@ def tile_picked_grand_relu_e_kernel(
             nc.vector.quantize_mx(
                 out=codes[:, cols].bitcast(FP8X4),
                 scales=scales[:, cols],
-                in_=xq[piece][:, 4 * first : 4 * (first + n)],
+                in_=xq[:, 4 * j0 : 4 * (j0 + n)],
             )
-            product(0, j0, n, f"mm{(piece, 4)[first > 0]}", on_vector)
-        for h in range(2):
-            product(1, h * 512, 512, f"mm{3 + h}", False)
+            relu(0, j0, n, product(0, j0, n, f"mm{(piece, 4)[first > 0]}"), on_vector)
+        upper = product(1, 512, 512, "mm3")
+        lower = product(1, 0, 512, "mm2")
+        relu(1, 512, 512, upper, False)
+        gc = keep.tile([P, V], F32, name="gc", tag="codes", align_bytes=64)
+        nc.scalar.activation(out=gc[:], in_=g_sum[:], func=ACT.Copy, scale=-1.0, bias=1.0)
+        factors = (gates[:, 0, :], gates[:, 1, :], gc[:])
+        relu(1, 0, 512, lower, False)
 
         def term(b, d, v0, v1):
             got = keep.tile([P, v1 - v0], F32, name=f"got{b}_{d}_{v0}")
@@ -198,8 +201,16 @@ def tile_picked_grand_relu_e_kernel(
         sum_by_transposes(0, 0, V, "fw0", "bk0")
         sum_by_transposes(1, 0, V // 2, "mm0", "bk1")
         last = [term(1, d, V // 2, V) for d in range(3)]
-        part = keep.tile([P, V // 2], F32, name="part")
-        nc.vector.tensor_tensor(out=part[:], in0=last[0][:], in1=last[1][:], op=ALU.add)
-        res = keep.tile([P, V // 2], F32, name="res_last")
-        nc.vector.tensor_tensor(out=res[:], in0=part[:], in1=last[2][:], op=ALU.add)
-        nc.sync.dma_start(out=out[P : 2 * P, V // 2 : V], in_=res[:])
+        quarter = V // 4
+        parts = []
+        for i in range(2):
+            cols = slice(i * quarter, (i + 1) * quarter)
+            part = keep.tile([P, quarter], F32, name=f"part{i}")
+            nc.vector.tensor_tensor(out=part[:], in0=last[0][:, cols], in1=last[1][:, cols], op=ALU.add)
+            parts.append(part)
+        for i in range(2):
+            cols = slice(i * quarter, (i + 1) * quarter)
+            res = keep.tile([P, quarter], F32, name=f"res_last{i}")
+            nc.vector.tensor_tensor(out=res[:], in0=parts[i][:], in1=last[2][:, cols], op=ALU.add)
+            v0 = V // 2 + i * quarter
+            nc.sync.dma_start(out=out[P : 2 * P, v0 : v0 + quarter], in_=res[:])

@@ -59,8 +59,14 @@ def tile_picked_grand_relu_e_kernel(
             nc.sync.dma_start(out=raw3[:, c0 : c0 + w], in_=x_rows[:, 3, c0 : c0 + w])
             c0 = c0 + w
 
-        w_words = keep.tile([P, 2 * N], U8, name="w_words", align_bytes=64)
-        nc.sync.dma_start(out=w_words[:].bitcast(I32), in_=w1_words[0].bitcast(I32))
+        w_words = [keep.tile([P, 2 * P], U8, name=f"w_words{b}", align_bytes=64) for b in range(2)]
+
+        def load_words(b):
+            nc.sync.dma_start(
+                out=w_words[b][:].bitcast(I32), in_=w1_words[0, :, 2 * P * b : 2 * P * (b + 1)].bitcast(I32)
+            )
+
+        load_words(0)
         w_scale = keep.tile([P, N], U8, name="w_scale", align_bytes=64)
         nc.gpsimd.memset(w_scale[:], 0)
         for q in range(4):
@@ -70,6 +76,7 @@ def tile_picked_grand_relu_e_kernel(
             )
         gates = keep.tile([P, 2, V], F32, name="gates")
         nc.sync.dma_start(out=gates[:], in_=gate.rearrange("d p v -> p d v"))
+        load_words(1)
         lists = []
         for name, src in (("pos1_t", pos1), ("pos2_t", pos2), ("cen_t", cen)):
             lst = keep.tile([P, V // 16], U16, name=name)
@@ -112,7 +119,7 @@ def tile_picked_grand_relu_e_kernel(
             acc = psum.tile([P, n], F32, name=f"acc{b}_{j0}", tag=bank)
             nc.tensor.matmul_mx(
                 out=acc[:],
-                lhsT=w_words[:, 2 * P * b : 2 * P * (b + 1)].bitcast(FP4X4),
+                lhsT=w_words[b][:].bitcast(FP4X4),
                 lhsT_scale=w_scale[:, P * b : P * (b + 1)],
                 rhs=codes[:, j0 : j0 + n].bitcast(FP8X4),
                 rhs_scale=scales[:, j0 : j0 + n],
@@ -155,12 +162,12 @@ def tile_picked_grand_relu_e_kernel(
                 in_=xq[:, 4 * j0 : 4 * (j0 + n)],
             )
             relu(0, j0, n, product(0, j0, n, f"mm{(piece, 4)[first > 0]}"), on_vector)
-        upper = product(1, 512, 512, "mm3")
-        lower = product(1, 0, 512, "mm2")
-        relu(1, 512, 512, upper, False)
-        gc = keep.tile([P, V], F32, name="gc", tag="codes", align_bytes=64)
+        gc = keep.tile([P, V], F32, name="gc", tag="w_words0", align_bytes=64)
         nc.scalar.activation(out=gc[:], in_=g_sum[:], func=ACT.Copy, scale=-1.0, bias=1.0)
         factors = (gates[:, 0, :], gates[:, 1, :], gc[:])
+        upper = product(1, 512, 512, "mm1")
+        lower = product(1, 0, 512, "mm0")
+        relu(1, 512, 512, upper, False)
         relu(1, 0, 512, lower, False)
 
         def term(b, d, v0, v1):
@@ -173,44 +180,48 @@ def tile_picked_grand_relu_e_kernel(
             )
             return got
 
-        def sum_by_transposes(b, v0, v1, fw_bank, bk_bank):
-            n = v1 - v0
-            turned = psum.tile([P, n], F32, name=f"turned{b}", tag=fw_bank)
+        def sum_by_transposes(b, v0, v1, banks):
+            n = (v1 - v0) // len(banks)
+            turned = [
+                psum.tile([P, n], F32, name=f"turned{b}_{v0}_{r}", tag=fw) for r, (fw, bk) in enumerate(banks)
+            ]
             for d in range(3):
                 got = term(b, d, v0, v1)
+                for r in range(len(banks)):
+                    for c in range(n // P):
+                        nc.tensor.matmul(
+                            turned[r][:, c * P : (c + 1) * P],
+                            got[:, r * n + c * P : r * n + (c + 1) * P],
+                            ident[:],
+                            start=(d == 0 and c == 0),
+                            stop=(d == 2 and c == n // P - 1),
+                            is_transpose=True,
+                        )
+            summed = []
+            for r in range(len(banks)):
+                t = keep.tile([P, n], F32, name=f"summed{b}_{v0}_{r}")
+                nc.scalar.copy(out=t[:], in_=turned[r][:])
+                summed.append(t)
+            res = keep.tile([P, v1 - v0], F32, name=f"res{b}_{v0}")
+            for r, (fw, bk) in enumerate(banks):
+                back = psum.tile([P, n], F32, name=f"back{b}_{v0}_{r}", tag=bk)
                 for c in range(n // P):
                     cols = slice(c * P, (c + 1) * P)
-                    nc.tensor.matmul(
-                        turned[:, cols],
-                        got[:, cols],
-                        ident[:],
-                        start=(d == 0 and c == 0),
-                        stop=(d == 2 and c == n // P - 1),
-                        is_transpose=True,
-                    )
-            summed = keep.tile([P, n], F32, name=f"summed{b}")
-            nc.scalar.copy(out=summed[:], in_=turned[:])
-            back = psum.tile([P, n], F32, name=f"back{b}", tag=bk_bank)
-            for c in range(n // P):
-                cols = slice(c * P, (c + 1) * P)
-                nc.tensor.transpose(back[:, cols], summed[:, cols], ident[:])
-            res = keep.tile([P, n], F32, name=f"res{b}")
-            nc.scalar.copy(out=res[:], in_=back[:])
-            nc.scalar.dma_start(out=out[P * b : P * (b + 1), v0:v1], in_=res[:])
+                    nc.tensor.transpose(back[:, cols], summed[r][:, cols], ident[:])
+                nc.scalar.copy(out=res[:, r * n : (r + 1) * n], in_=back[:])
+            (nc.sync, nc.scalar)[b].dma_start(out=out[P * b : P * (b + 1), v0:v1], in_=res[:])
 
-        sum_by_transposes(0, 0, V, "fw0", "bk0")
-        sum_by_transposes(1, 0, V // 2, "mm0", "bk1")
-        last = [term(1, d, V // 2, V) for d in range(3)]
-        quarter = V // 4
+        sum_by_transposes(0, 0, V // 2, (("fw0", "bk0"),))
+        sum_by_transposes(0, V // 2, V, (("mm2", "mm3"),))
+        sum_by_transposes(1, 0, P, (("mm4", "bk1"),))
+        last = [term(1, d, P, V) for d in range(3)]
+        runs = ((0, 192), (192, 384))
         parts = []
-        for i in range(2):
-            cols = slice(i * quarter, (i + 1) * quarter)
-            part = keep.tile([P, quarter], F32, name=f"part{i}")
-            nc.vector.tensor_tensor(out=part[:], in0=last[0][:, cols], in1=last[1][:, cols], op=ALU.add)
+        for c0, c1 in runs:
+            part = keep.tile([P, c1 - c0], F32, name=f"part{c0}")
+            nc.vector.tensor_tensor(out=part[:], in0=last[0][:, c0:c1], in1=last[1][:, c0:c1], op=ALU.add)
             parts.append(part)
-        for i in range(2):
-            cols = slice(i * quarter, (i + 1) * quarter)
-            res = keep.tile([P, quarter], F32, name=f"res_last{i}")
-            nc.vector.tensor_tensor(out=res[:], in0=parts[i][:], in1=last[2][:, cols], op=ALU.add)
-            v0 = V // 2 + i * quarter
-            nc.sync.dma_start(out=out[P : 2 * P, v0 : v0 + quarter], in_=res[:])
+        for (c0, c1), part in zip(runs, parts):
+            res = keep.tile([P, c1 - c0], F32, name=f"res_last{c0}")
+            nc.vector.tensor_tensor(out=res[:], in0=part[:], in1=last[2][:, c0:c1], op=ALU.add)
+            nc.sync.dma_start(out=out[P : 2 * P, P + c0 : P + c1], in_=res[:])

@@ -18,9 +18,8 @@ FP4X4 = mybir.dt.float4_e2m1fn_x4
 ALU = mybir.AluOpType
 ACT = mybir.ActivationFunctionType
 
-PAIR_CHUNKS = (1024, 768, 256)
-V_SHARE = (224, 512, 160)
-LAST_CHUNKS = (640, 544, 480, 384)
+CHUNKS = ((1024, 1024), (640, 640, 576, 192))
+V_SHARE = ((672, 672), (0, 320, 384, 128))
 PIECE = 256
 PIECES = S // PIECE
 VCH = V // P
@@ -42,22 +41,17 @@ def tile_picked_grand_relu_e_kernel(
         make_identity(nc, ident[:])
 
         x_rows = xT.rearrange("(p j) t -> p j t", j=4)
-        raw2 = keep.tile([P, T], F32, name="raw2")
-        nc.sync.dma_start(out=raw2[:], in_=x_rows[:, 2, :])
-        offs_t = keep.tile([P, S // 16], U16, name="offs_t")
-        nc.sync.dma_start(offs_t[:], offs)
         raws = []
-        c0 = 0
-        for i, w in enumerate(PAIR_CHUNKS):
-            raw = keep.tile([P, 2, w], F32, name=f"raw01_{i}", tag=("raw0", "raw1", "single")[i])
-            nc.sync.dma_start(out=raw[:], in_=x_rows[:, 0:2, c0 : c0 + w])
-            raws.append((i, c0, w, raw))
-            c0 = c0 + w
-        raw3 = keep.tile([P, T], F32, name="raw3")
-        c0 = 0
-        for w in LAST_CHUNKS:
-            nc.sync.dma_start(out=raw3[:, c0 : c0 + w], in_=x_rows[:, 3, c0 : c0 + w])
-            c0 = c0 + w
+        offs_t = keep.tile([P, S // 16], U16, name="offs_t")
+        for u in range(2):
+            c0 = 0
+            for i, w in enumerate(CHUNKS[u]):
+                raw = keep.tile([P, 2, w], F32, name=f"raw{u}_{i}")
+                nc.sync.dma_start(out=raw[:], in_=x_rows[:, 2 * u : 2 * u + 2, c0 : c0 + w])
+                raws.append((u, i, c0, w, raw))
+                c0 = c0 + w
+            if u == 0:
+                nc.sync.dma_start(offs_t[:], offs)
 
         w_words = [keep.tile([P, 2 * P], U8, name=f"w_words{b}", align_bytes=64) for b in range(2)]
 
@@ -99,19 +93,26 @@ def tile_picked_grand_relu_e_kernel(
                     is_transpose=True,
                 )
 
-        pair = keep.tile([P, 2 * T], BF16, name="pair")
-        plane3 = keep.tile([P, T], BF16, name="plane3", tag="single")
-        xq = keep.tile([P, 4 * S], BF16, name="xq", align_bytes=64)
-        xq_slots = xq[:].rearrange("p (c t) -> p c t", t=4)
-        xq_words = xq[:].bitcast(U32).rearrange("p (c u) -> p c u", u=2)
+        pairs = [keep.tile([P, 2 * T], BF16, name=f"pair{u}") for u in range(2)]
+        picked = [keep.tile([P, 2, PIECE], U32, name=f"picked{i}") for i in range(PIECES)]
+        xq = [keep.tile([P, 2 * PIECE], U32, name=f"xq{i}", align_bytes=64) for i in range(PIECES)]
 
-        def entries(i):
-            return offs_t[:, i * PIECE // 16 : (i + 1) * PIECE // 16]
+        def cast(u, i, c0, w, raw):
+            vs = V_SHARE[u][i]
+            dst = pairs[u][:, 2 * c0 : 2 * (c0 + w)].rearrange("p (t e) -> p t e", e=2)
+            src = raw[:].rearrange("p e t -> p t e")
+            if vs > 0:
+                nc.vector.tensor_copy(out=dst[:, 0:vs, :], in_=src[:, 0:vs, :])
+            if vs < w:
+                nc.scalar.copy(out=dst[:, vs:w, :], in_=src[:, vs:w, :])
 
-        def slot(i, t):
-            return xq_slots[:, i * PIECE : (i + 1) * PIECE, t]
+        def gather(u, i):
+            nc.vector.tensor_copy(
+                out=picked[i][:, u, :],
+                in_=pairs[u][:].bitcast(U32).indirect(offs_t[:, i * PIECE // 16 : (i + 1) * PIECE // 16]),
+            )
 
-        y = [keep.tile([P, S], F32, name=f"y{b}", tag=("single", "y1")[b]) for b in range(2)]
+        y = [keep.tile([P, S], F32, name=f"y{b}") for b in range(2)]
         codes = keep.tile([P, S], U32, name="codes", align_bytes=64)
         scales = keep.tile([P, S], U8, name="scales", align_bytes=64)
 
@@ -134,39 +135,35 @@ def tile_picked_grand_relu_e_kernel(
             else:
                 nc.scalar.activation(out=y[b][:, j0 : j0 + n], in_=acc[:], func=ACT.Relu)
 
-        nc.vector.tensor_copy(out=xq_slots[:, :, 2], in_=raw2[:].indirect(offs_t[:]))
-        for i, c0, w, raw in raws:
-            vs = V_SHARE[i]
-            dst = pair[:, 2 * c0 : 2 * (c0 + w)].rearrange("p (t e) -> p t e", e=2)
-            src = raw[:].rearrange("p e t -> p t e")
-            nc.scalar.copy(out=dst[:, vs:w, :], in_=src[:, vs:w, :])
-            nc.vector.tensor_copy(out=dst[:, 0:vs, :], in_=src[:, 0:vs, :])
+        for r in raws:
+            if r[0] == 0:
+                cast(*r)
         for i in range(PIECES):
-            nc.vector.tensor_copy(
-                out=xq_words[:, i * PIECE : (i + 1) * PIECE, 0],
-                in_=pair[:].bitcast(U32).indirect(entries(i)),
+            gather(0, i)
+        for r in raws:
+            if r[0] == 1:
+                cast(*r)
+        for i in range(PIECES):
+            gather(1, i)
+            nc.scalar.copy(
+                out=xq[i][:].rearrange("p (c u) -> p c u", u=2), in_=picked[i][:].rearrange("p u c -> p c u")
             )
-        c0 = 0
-        for w in LAST_CHUNKS:
-            nc.scalar.copy(out=plane3[:, c0 : c0 + w], in_=raw3[:, c0 : c0 + w])
-            c0 = c0 + w
-        for i in range(PIECES - 1):
-            nc.scalar.activation(out=slot(i, 3), in_=plane3[:].indirect(entries(i)), func=ACT.Copy)
-        nc.vector.tensor_copy(out=slot(PIECES - 1, 3), in_=raw3[:].indirect(entries(PIECES - 1)))
-        for piece, first, n, on_vector in ((0, 0, 256, False), (1, 0, 256, False), (3, 0, 256, False), (2, 0, 128, True), (2, 128, 128, True)):
-            j0 = piece * PIECE + first
+        j0 = 0
+        for i, n in enumerate((256, 256, 256, 128, 128)):
             cols = slice(j0, j0 + n)
+            piece, first = divmod(j0, PIECE)
             nc.vector.quantize_mx(
                 out=codes[:, cols].bitcast(FP8X4),
                 scales=scales[:, cols],
-                in_=xq[:, 4 * j0 : 4 * (j0 + n)],
+                in_=xq[piece][:, 2 * first : 2 * (first + n)].bitcast(BF16),
             )
-            relu(0, j0, n, product(0, j0, n, f"mm{(piece, 4)[first > 0]}"), on_vector)
+            relu(0, j0, n, product(0, j0, n, f"mm{i}"), i == 3)
+            j0 = j0 + n
         gc = keep.tile([P, V], F32, name="gc", tag="w_words0", align_bytes=64)
         nc.scalar.activation(out=gc[:], in_=g_sum[:], func=ACT.Copy, scale=-1.0, bias=1.0)
         factors = (gates[:, 0, :], gates[:, 1, :], gc[:])
-        upper = product(1, 512, 512, "mm1")
-        lower = product(1, 0, 512, "mm0")
+        upper = product(1, 512, 512, "mm4")
+        lower = product(1, 0, 512, "mm2")
         relu(1, 512, 512, upper, False)
         relu(1, 0, 512, lower, False)
 
@@ -212,8 +209,8 @@ def tile_picked_grand_relu_e_kernel(
             (nc.sync, nc.scalar)[b].dma_start(out=out[P * b : P * (b + 1), v0:v1], in_=res[:])
 
         sum_by_transposes(0, 0, V // 2, (("fw0", "bk0"),))
-        sum_by_transposes(0, V // 2, V, (("mm2", "mm3"),))
-        sum_by_transposes(1, 0, P, (("mm4", "bk1"),))
+        sum_by_transposes(0, V // 2, V, (("mm0", "mm1"),))
+        sum_by_transposes(1, 0, P, (("mm3", "bk1"),))
         last = [term(1, d, P, V) for d in range(3)]
         runs = ((0, 192), (192, 384))
         parts = []

@@ -19,10 +19,14 @@ ALU = mybir.AluOpType
 ACT = mybir.ActivationFunctionType
 
 CHUNKS = ((1024, 1024), (640, 640, 576, 192))
-V_SHARE = ((672, 672), (0, 320, 384, 128))
+VECTOR_COLUMNS = ((672, 672), (0, 320, 384, 128))
 PIECE = 256
 PIECES = S // PIECE
-VCH = V // P
+QUANTISED = (256, 256, 256, 128, 128)
+RELU_ON_VECTOR = 2
+GATE_CHUNKS = V // P
+TURNED_LAST = P
+HALF_LAST = (V - TURNED_LAST) // 2
 
 
 def tile_picked_grand_relu_e_kernel(
@@ -33,23 +37,24 @@ def tile_picked_grand_relu_e_kernel(
         keep = ctx.enter_context(tc.tile_pool(name="keep", bufs=1))
         psum = ctx.enter_context(tc.psum_pool(name="psum", bufs=1))
 
-        g_rows = keep.tile([P, P], F32, name="g_rows")
-        nc.gpsimd.memset(g_rows[0 : P - 2 * VCH, :], 0.0)
-        gate_chunks = gate.rearrange("d p (c v) -> (d p c) v", v=P)
-        nc.scalar.dma_start(out=g_rows[P - 2 * VCH : P, :], in_=gate_chunks[0 :: 32 * VCH + 1, :])
+        gate_rows = keep.tile([P, P], F32, name="gate_rows")
+        first_row = P - 2 * GATE_CHUNKS
+        nc.gpsimd.memset(gate_rows[0:first_row, :], 0.0)
+        gate_runs = gate.rearrange("d p (c v) -> (d p c) v", v=P)
+        nc.scalar.dma_start(out=gate_rows[first_row:P, :], in_=gate_runs[0 :: 32 * GATE_CHUNKS + 1, :])
         ident = keep.tile([P, P], F32, name="ident")
         make_identity(nc, ident[:])
 
         x_rows = xT.rearrange("(p j) t -> p j t", j=4)
-        raws = []
         offs_t = keep.tile([P, S // 16], U16, name="offs_t")
+        loads = ([], [])
         for u in range(2):
             c0 = 0
-            for i, w in enumerate(CHUNKS[u]):
-                raw = keep.tile([P, 2, w], F32, name=f"raw{u}_{i}")
-                nc.sync.dma_start(out=raw[:], in_=x_rows[:, 2 * u : 2 * u + 2, c0 : c0 + w])
-                raws.append((u, i, c0, w, raw))
-                c0 = c0 + w
+            for width, on_vector in zip(CHUNKS[u], VECTOR_COLUMNS[u]):
+                raw = keep.tile([P, 2, width], F32, name=f"raw{u}_{c0}")
+                nc.sync.dma_start(out=raw[:], in_=x_rows[:, 2 * u : 2 * u + 2, c0 : c0 + width])
+                loads[u].append((raw, c0, width, on_vector))
+                c0 = c0 + width
             if u == 0:
                 nc.sync.dma_start(offs_t[:], offs)
 
@@ -76,45 +81,50 @@ def tile_picked_grand_relu_e_kernel(
             lst = keep.tile([P, V // 16], U16, name=name)
             nc.sync.dma_start(lst[:], src)
             lists.append(lst)
-        g_turned = psum.tile([P, P], F32, name="g_turned", tag="bk0")
-        nc.tensor.transpose(g_turned[:], g_rows[:], ident[:])
-        g_cols = keep.tile([P, 2 * VCH], F32, name="g_cols")
-        nc.scalar.copy(out=g_cols[:], in_=g_turned[:, P - 2 * VCH : P])
-        g_sum = psum.tile([P, V], F32, name="g_sum", tag="bk1")
+
+        gate_turned = psum.tile([P, P], F32, name="gate_turned", tag="bank6")
+        nc.tensor.transpose(gate_turned[:], gate_rows[:], ident[:])
+        gate_cols = keep.tile([P, 2 * GATE_CHUNKS], F32, name="gate_cols")
+        nc.scalar.copy(out=gate_cols[:], in_=gate_turned[:, first_row:P])
+        gate_sum = psum.tile([P, V], F32, name="gate_sum", tag="bank7")
         for d in range(2):
-            for c in range(VCH):
-                col = VCH * d + c
+            for c in range(GATE_CHUNKS):
+                col = GATE_CHUNKS * d + c
                 nc.tensor.matmul(
-                    g_sum[:, c * P : (c + 1) * P],
-                    g_cols[:, col : col + 1].to_broadcast([P, P]),
+                    gate_sum[:, c * P : (c + 1) * P],
+                    gate_cols[:, col : col + 1].to_broadcast([P, P]),
                     ident[:],
                     start=(d == 0 and c == 0),
-                    stop=(d == 1 and c == VCH - 1),
+                    stop=(d == 1 and c == GATE_CHUNKS - 1),
                     is_transpose=True,
                 )
 
         pairs = [keep.tile([P, 2 * T], BF16, name=f"pair{u}") for u in range(2)]
         picked = [keep.tile([P, 2, PIECE], U32, name=f"picked{i}") for i in range(PIECES)]
-        xq = [keep.tile([P, 2 * PIECE], U32, name=f"xq{i}", align_bytes=64) for i in range(PIECES)]
+        woven = [keep.tile([P, 2 * PIECE], U32, name=f"woven{i}", align_bytes=64) for i in range(PIECES)]
+        y = [keep.tile([P, S], F32, name=f"y{b}") for b in range(2)]
+        codes = keep.tile([P, S], U32, name="codes", align_bytes=64)
+        scales = keep.tile([P, S], U8, name="scales", align_bytes=64)
 
-        def cast(u, i, c0, w, raw):
-            vs = V_SHARE[u][i]
-            dst = pairs[u][:, 2 * c0 : 2 * (c0 + w)].rearrange("p (t e) -> p t e", e=2)
-            src = raw[:].rearrange("p e t -> p t e")
-            if vs > 0:
-                nc.vector.tensor_copy(out=dst[:, 0:vs, :], in_=src[:, 0:vs, :])
-            if vs < w:
-                nc.scalar.copy(out=dst[:, vs:w, :], in_=src[:, vs:w, :])
+        def round_pair(u):
+            for raw, c0, width, on_vector in loads[u]:
+                dst = pairs[u][:, 2 * c0 : 2 * (c0 + width)].rearrange("p (t e) -> p t e", e=2)
+                src = raw[:].rearrange("p e t -> p t e")
+                if on_vector > 0:
+                    nc.vector.tensor_copy(out=dst[:, 0:on_vector, :], in_=src[:, 0:on_vector, :])
+                nc.scalar.copy(out=dst[:, on_vector:width, :], in_=src[:, on_vector:width, :])
 
-        def gather(u, i):
+        def gather_pair(u, i):
             nc.vector.tensor_copy(
                 out=picked[i][:, u, :],
                 in_=pairs[u][:].bitcast(U32).indirect(offs_t[:, i * PIECE // 16 : (i + 1) * PIECE // 16]),
             )
 
-        y = [keep.tile([P, S], F32, name=f"y{b}") for b in range(2)]
-        codes = keep.tile([P, S], U32, name="codes", align_bytes=64)
-        scales = keep.tile([P, S], U8, name="scales", align_bytes=64)
+        def weave(i, c0, c1):
+            nc.scalar.copy(
+                out=woven[i][:].rearrange("p (c u) -> p c u", u=2)[:, c0:c1, :],
+                in_=picked[i][:].rearrange("p u c -> p c u")[:, c0:c1, :],
+            )
 
         def product(b, j0, n, bank):
             acc = psum.tile([P, n], F32, name=f"acc{b}_{j0}", tag=bank)
@@ -129,46 +139,45 @@ def tile_picked_grand_relu_e_kernel(
             )
             return acc
 
-        def relu(b, j0, n, acc, on_vector):
-            if on_vector:
-                nc.vector.tensor_scalar_max(out=y[b][:, j0 : j0 + n], in0=acc[:], scalar1=0.0)
-            else:
-                nc.scalar.activation(out=y[b][:, j0 : j0 + n], in_=acc[:], func=ACT.Relu)
+        def relu_on_scalar(b, j0, n, acc):
+            nc.scalar.activation(out=y[b][:, j0 : j0 + n], in_=acc[:], func=ACT.Relu)
 
-        for r in raws:
-            if r[0] == 0:
-                cast(*r)
+        round_pair(0)
         for i in range(PIECES):
-            gather(0, i)
-        for r in raws:
-            if r[0] == 1:
-                cast(*r)
-        for i in range(PIECES):
-            gather(1, i)
-            nc.scalar.copy(
-                out=xq[i][:].rearrange("p (c u) -> p c u", u=2), in_=picked[i][:].rearrange("p u c -> p c u")
-            )
+            gather_pair(0, i)
+        round_pair(1)
+        for i in range(PIECES - 1):
+            gather_pair(1, i)
+            weave(i, 0, PIECE)
+        gather_pair(1, PIECES - 1)
+        weave(PIECES - 1, 0, PIECE // 2)
+        weave(PIECES - 1, PIECE // 2, PIECE)
+
         j0 = 0
-        for i, n in enumerate((256, 256, 256, 128, 128)):
-            cols = slice(j0, j0 + n)
+        for i, n in enumerate(QUANTISED):
             piece, first = divmod(j0, PIECE)
             nc.vector.quantize_mx(
-                out=codes[:, cols].bitcast(FP8X4),
-                scales=scales[:, cols],
-                in_=xq[piece][:, 2 * first : 2 * (first + n)].bitcast(BF16),
+                out=codes[:, j0 : j0 + n].bitcast(FP8X4),
+                scales=scales[:, j0 : j0 + n],
+                in_=woven[piece][:, 2 * first : 2 * (first + n)].bitcast(BF16),
             )
-            relu(0, j0, n, product(0, j0, n, f"mm{i}"), i == 3)
+            acc = product(0, j0, n, f"bank{i}")
+            if i == RELU_ON_VECTOR:
+                nc.vector.tensor_scalar_max(out=y[0][:, j0 : j0 + n], in0=acc[:], scalar1=0.0)
+            else:
+                relu_on_scalar(0, j0, n, acc)
             j0 = j0 + n
-        gc = keep.tile([P, V], F32, name="gc", tag="w_words0", align_bytes=64)
-        nc.scalar.activation(out=gc[:], in_=g_sum[:], func=ACT.Copy, scale=-1.0, bias=1.0)
-        factors = (gates[:, 0, :], gates[:, 1, :], gc[:])
-        upper = product(1, 512, 512, "mm4")
-        lower = product(1, 0, 512, "mm2")
-        relu(1, 512, 512, upper, False)
-        relu(1, 0, 512, lower, False)
+
+        centre = keep.tile([P, V], F32, name="centre", tag="w_words0", align_bytes=64)
+        nc.scalar.activation(out=centre[:], in_=gate_sum[:], func=ACT.Copy, scale=-1.0, bias=1.0)
+        factors = (gates[:, 0, :], gates[:, 1, :], centre[:])
+        upper = product(1, S // 2, S // 2, "bank4")
+        lower = product(1, 0, S // 2, "bank2")
+        relu_on_scalar(1, S // 2, S // 2, upper)
+        relu_on_scalar(1, 0, S // 2, lower)
 
         def term(b, d, v0, v1):
-            got = keep.tile([P, v1 - v0], F32, name=f"got{b}_{d}_{v0}")
+            got = keep.tile([P, v1 - v0], F32, name=f"term{b}_{d}_{v0}")
             nc.vector.tensor_tensor(
                 out=got[:],
                 in0=y[b][:].indirect(lists[d][:, v0 // 16 : v1 // 16]),
@@ -177,48 +186,43 @@ def tile_picked_grand_relu_e_kernel(
             )
             return got
 
-        def sum_by_transposes(b, v0, v1, banks):
-            n = (v1 - v0) // len(banks)
-            turned = [
-                psum.tile([P, n], F32, name=f"turned{b}_{v0}_{r}", tag=fw) for r, (fw, bk) in enumerate(banks)
-            ]
+        def sum_by_transposes(b, v0, v1, bank_there, bank_back, queue):
+            n = v1 - v0
+            blocks = [slice(c, c + P) for c in range(0, n, P)]
+            turned = psum.tile([P, n], F32, name=f"turned{b}_{v0}", tag=bank_there)
             for d in range(3):
                 got = term(b, d, v0, v1)
-                for r in range(len(banks)):
-                    for c in range(n // P):
-                        nc.tensor.matmul(
-                            turned[r][:, c * P : (c + 1) * P],
-                            got[:, r * n + c * P : r * n + (c + 1) * P],
-                            ident[:],
-                            start=(d == 0 and c == 0),
-                            stop=(d == 2 and c == n // P - 1),
-                            is_transpose=True,
-                        )
-            summed = []
-            for r in range(len(banks)):
-                t = keep.tile([P, n], F32, name=f"summed{b}_{v0}_{r}")
-                nc.scalar.copy(out=t[:], in_=turned[r][:])
-                summed.append(t)
-            res = keep.tile([P, v1 - v0], F32, name=f"res{b}_{v0}")
-            for r, (fw, bk) in enumerate(banks):
-                back = psum.tile([P, n], F32, name=f"back{b}_{v0}_{r}", tag=bk)
-                for c in range(n // P):
-                    cols = slice(c * P, (c + 1) * P)
-                    nc.tensor.transpose(back[:, cols], summed[r][:, cols], ident[:])
-                nc.scalar.copy(out=res[:, r * n : (r + 1) * n], in_=back[:])
-            (nc.sync, nc.scalar)[b].dma_start(out=out[P * b : P * (b + 1), v0:v1], in_=res[:])
+                for c, cols in enumerate(blocks):
+                    nc.tensor.matmul(
+                        turned[:, cols],
+                        got[:, cols],
+                        ident[:],
+                        start=(d == 0 and c == 0),
+                        stop=(d == 2 and c == len(blocks) - 1),
+                        is_transpose=True,
+                    )
+            summed = keep.tile([P, n], F32, name=f"summed{b}_{v0}")
+            nc.scalar.copy(out=summed[:], in_=turned[:])
+            res = keep.tile([P, n], F32, name=f"res{b}_{v0}")
+            back = psum.tile([P, n], F32, name=f"back{b}_{v0}", tag=bank_back)
+            for cols in blocks:
+                nc.tensor.transpose(back[:, cols], summed[:, cols], ident[:])
+            nc.scalar.copy(out=res[:], in_=back[:])
+            queue.dma_start(out=out[P * b : P * (b + 1), v0:v1], in_=res[:])
 
-        sum_by_transposes(0, 0, V // 2, (("fw0", "bk0"),))
-        sum_by_transposes(0, V // 2, V, (("mm0", "mm1"),))
-        sum_by_transposes(1, 0, P, (("mm3", "bk1"),))
-        last = [term(1, d, P, V) for d in range(3)]
-        runs = ((0, 192), (192, 384))
-        parts = []
-        for c0, c1 in runs:
-            part = keep.tile([P, c1 - c0], F32, name=f"part{c0}")
-            nc.vector.tensor_tensor(out=part[:], in0=last[0][:, c0:c1], in1=last[1][:, c0:c1], op=ALU.add)
-            parts.append(part)
-        for (c0, c1), part in zip(runs, parts):
-            res = keep.tile([P, c1 - c0], F32, name=f"res_last{c0}")
-            nc.vector.tensor_tensor(out=res[:], in0=part[:], in1=last[2][:, c0:c1], op=ALU.add)
-            nc.sync.dma_start(out=out[P : 2 * P, P + c0 : P + c1], in_=res[:])
+        sum_by_transposes(0, 0, V // 2, "bank5", "bank6", nc.sync)
+        sum_by_transposes(0, V // 2, V, "bank0", "bank1", nc.sync)
+        sum_by_transposes(1, 0, TURNED_LAST, "bank3", "bank7", nc.scalar)
+
+        last = [term(1, d, TURNED_LAST, V) for d in range(3)]
+        halves = [slice(h * HALF_LAST, (h + 1) * HALF_LAST) for h in range(2)]
+        two_terms = []
+        for h, cols in enumerate(halves):
+            part = keep.tile([P, HALF_LAST], F32, name=f"two_terms{h}")
+            nc.vector.tensor_tensor(out=part[:], in0=last[0][:, cols], in1=last[1][:, cols], op=ALU.add)
+            two_terms.append(part)
+        for h, cols in enumerate(halves):
+            res = keep.tile([P, HALF_LAST], F32, name=f"res_last{h}")
+            nc.vector.tensor_tensor(out=res[:], in0=two_terms[h][:], in1=last[2][:, cols], op=ALU.add)
+            v0 = TURNED_LAST + h * HALF_LAST
+            nc.sync.dma_start(out=out[P : 2 * P, v0 : v0 + HALF_LAST], in_=res[:])

@@ -18,15 +18,9 @@ FP4X4 = mybir.dt.float4_e2m1fn_x4
 ALU = mybir.AluOpType
 ACT = mybir.ActivationFunctionType
 
-CHUNKS = ((1024, 1024), (640, 640, 576, 192))
-VECTOR_COLUMNS = ((672, 672), (0, 320, 384, 128))
 PIECE = 256
 PIECES = S // PIECE
-QUANTISED = (256, 256, 256, 128, 128)
-RELU_ON_VECTOR = 2
 GATE_CHUNKS = V // P
-TURNED_LAST = P
-HALF_LAST = (V - TURNED_LAST) // 2
 
 
 def tile_picked_grand_relu_e_kernel(
@@ -37,35 +31,30 @@ def tile_picked_grand_relu_e_kernel(
         keep = ctx.enter_context(tc.tile_pool(name="keep", bufs=1))
         psum = ctx.enter_context(tc.psum_pool(name="psum", bufs=1))
 
-        gate_rows = keep.tile([P, P], F32, name="gate_rows")
-        first_row = P - 2 * GATE_CHUNKS
-        nc.gpsimd.memset(gate_rows[0:first_row, :], 0.0)
-        gate_runs = gate.rearrange("d p (c v) -> (d p c) v", v=P)
-        nc.scalar.dma_start(out=gate_rows[first_row:P, :], in_=gate_runs[0 :: 32 * GATE_CHUNKS + 1, :])
+        gate_rows = keep.tile([P, 2, P], F32, name="gate_rows")
+        first_row = P - GATE_CHUNKS
+        zero = keep.tile([P, 1], F32, name="zero")
+        nc.vector.memset(zero[:], 0.0)
+        nc.scalar.copy(
+            out=gate_rows[0:first_row, :, :].rearrange("p d v -> p (d v)"),
+            in_=zero[0:first_row, :].to_broadcast([first_row, 2 * P]),
+        )
+        nc.scalar.dma_start(out=gate_rows[first_row:P, :, :], in_=gate[:, 0, :].rearrange("d (c v) -> c d v", v=P))
         ident = keep.tile([P, P], F32, name="ident")
         make_identity(nc, ident[:])
 
         x_rows = xT.rearrange("(p j) t -> p j t", j=4)
         offs_t = keep.tile([P, S // 16], U16, name="offs_t")
-        loads = ([], [])
-        for u in range(2):
-            c0 = 0
-            for width, on_vector in zip(CHUNKS[u], VECTOR_COLUMNS[u]):
-                raw = keep.tile([P, 2, width], F32, name=f"raw{u}_{c0}")
-                nc.sync.dma_start(out=raw[:], in_=x_rows[:, 2 * u : 2 * u + 2, c0 : c0 + width])
-                loads[u].append((raw, c0, width, on_vector))
-                c0 = c0 + width
-            if u == 0:
+        rows = []
+        for j in range(4):
+            row = keep.tile([P, T], F32, name=f"row{j}")
+            nc.sync.dma_start(out=row[:], in_=x_rows[:, j, :])
+            rows.append(row)
+            if j == 0:
                 nc.sync.dma_start(offs_t[:], offs)
 
-        w_words = [keep.tile([P, 2 * P], U8, name=f"w_words{b}", align_bytes=64) for b in range(2)]
-
-        def load_words(b):
-            nc.sync.dma_start(
-                out=w_words[b][:].bitcast(I32), in_=w1_words[0, :, 2 * P * b : 2 * P * (b + 1)].bitcast(I32)
-            )
-
-        load_words(0)
+        w_words = keep.tile([P, 2 * N], U8, name="w_words", align_bytes=64)
+        nc.sync.dma_start(out=w_words[:].bitcast(I32), in_=w1_words[0].bitcast(I32))
         w_scale = keep.tile([P, N], U8, name="w_scale", align_bytes=64)
         nc.gpsimd.memset(w_scale[:], 0)
         for q in range(4):
@@ -75,106 +64,119 @@ def tile_picked_grand_relu_e_kernel(
             )
         gates = keep.tile([P, 2, V], F32, name="gates")
         nc.sync.dma_start(out=gates[:], in_=gate.rearrange("d p v -> p d v"))
-        load_words(1)
         lists = []
         for name, src in (("pos1_t", pos1), ("pos2_t", pos2), ("cen_t", cen)):
             lst = keep.tile([P, V // 16], U16, name=name)
             nc.sync.dma_start(lst[:], src)
             lists.append(lst)
 
-        gate_turned = psum.tile([P, P], F32, name="gate_turned", tag="bank6")
-        nc.tensor.transpose(gate_turned[:], gate_rows[:], ident[:])
-        gate_cols = keep.tile([P, 2 * GATE_CHUNKS], F32, name="gate_cols")
-        nc.scalar.copy(out=gate_cols[:], in_=gate_turned[:, first_row:P])
-        gate_sum = psum.tile([P, V], F32, name="gate_sum", tag="bank7")
+        gate_turned = psum.tile([P, 2, P], F32, name="gate_turned", tag="bank6")
+        nc.tensor.transpose(gate_turned[:, 0, :], gate_rows[:, 0, :], ident[:])
         for d in range(2):
-            for c in range(GATE_CHUNKS):
-                col = GATE_CHUNKS * d + c
-                nc.tensor.matmul(
-                    gate_sum[:, c * P : (c + 1) * P],
-                    gate_cols[:, col : col + 1].to_broadcast([P, P]),
-                    ident[:],
-                    start=(d == 0 and c == 0),
-                    stop=(d == 1 and c == GATE_CHUNKS - 1),
-                    is_transpose=True,
-                )
+            nc.tensor.matmul(
+                gate_turned[:, 1, :], gate_rows[:, d, :], ident[:], start=(d == 0), stop=(d == 1), is_transpose=True
+            )
+        first_cols = keep.tile([P, GATE_CHUNKS], F32, name="first_cols")
+        centre_cols = keep.tile([P, GATE_CHUNKS], F32, name="centre_cols")
+        nc.scalar.activation(
+            out=centre_cols[:], in_=gate_turned[:, 1, first_row:P], func=ACT.Copy, scale=-1.0, bias=1.0
+        )
+        nc.scalar.copy(out=first_cols[:], in_=gate_turned[:, 0, first_row:P])
+        centre_turned = psum.tile([P, V], F32, name="centre_turned", tag="bank7")
+        for c in range(GATE_CHUNKS):
+            nc.tensor.transpose(
+                centre_turned[:, c * P : (c + 1) * P], centre_cols[:, c : c + 1].to_broadcast([P, P]), ident[:]
+            )
+        centre = keep.tile([P, V], F32, name="centre")
+        nc.scalar.copy(out=centre[:], in_=centre_turned[:])
 
-        pairs = [keep.tile([P, 2 * T], BF16, name=f"pair{u}") for u in range(2)]
-        picked = [keep.tile([P, 2, PIECE], U32, name=f"picked{i}") for i in range(PIECES)]
-        woven = [keep.tile([P, 2 * PIECE], U32, name=f"woven{i}", align_bytes=64) for i in range(PIECES)]
+        woven = [keep.tile([P, PIECE, 4], BF16, name=f"woven{i}", align_bytes=64) for i in range(PIECES)]
+        early = keep.tile([P, 2, S - PIECE], BF16, name="early")
+        late = [keep.tile([P, 2, PIECE], BF16, name=f"late{i}") for i in range(1, PIECES)]
         y = [keep.tile([P, S], F32, name=f"y{b}") for b in range(2)]
+
+        def entries(j0, j1):
+            return offs_t[:, j0 // 16 : j1 // 16]
+
+        for j in range(4):
+            nc.vector.tensor_copy(out=woven[0][:, :, j], in_=rows[j][:].indirect(entries(0, PIECE)))
+            if j < 2:
+                nc.scalar.activation(out=early[:, j, :], in_=rows[j][:].indirect(entries(PIECE, S)), func=ACT.Copy)
+            else:
+                for i in range(1, PIECES):
+                    nc.scalar.activation(
+                        out=late[i - 1][:, j - 2, :],
+                        in_=rows[j][:].indirect(entries(i * PIECE, (i + 1) * PIECE)),
+                        func=ACT.Copy,
+                    )
+            if j == 1:
+                for i in range(1, PIECES):
+                    nc.vector.tensor_copy(
+                        out=woven[i][:, :, 0:2],
+                        in_=early[:, :, (i - 1) * PIECE : i * PIECE].rearrange("p j c -> p c j"),
+                    )
+
+        def place(engine_copy, i, c0, c1):
+            engine_copy(out=woven[i][:, c0:c1, 2:4], in_=late[i - 1][:, :, c0:c1].rearrange("p j c -> p c j"))
+
         codes = keep.tile([P, S], U32, name="codes", align_bytes=64)
         scales = keep.tile([P, S], U8, name="scales", align_bytes=64)
 
-        def round_pair(u):
-            for raw, c0, width, on_vector in loads[u]:
-                dst = pairs[u][:, 2 * c0 : 2 * (c0 + width)].rearrange("p (t e) -> p t e", e=2)
-                src = raw[:].rearrange("p e t -> p t e")
-                if on_vector > 0:
-                    nc.vector.tensor_copy(out=dst[:, 0:on_vector, :], in_=src[:, 0:on_vector, :])
-                nc.scalar.copy(out=dst[:, on_vector:width, :], in_=src[:, on_vector:width, :])
-
-        def gather_pair(u, i):
-            nc.vector.tensor_copy(
-                out=picked[i][:, u, :],
-                in_=pairs[u][:].bitcast(U32).indirect(offs_t[:, i * PIECE // 16 : (i + 1) * PIECE // 16]),
+        def quantise(j0, n):
+            piece, first = divmod(j0, PIECE)
+            nc.vector.quantize_mx(
+                out=codes[:, j0 : j0 + n].bitcast(FP8X4),
+                scales=scales[:, j0 : j0 + n],
+                in_=woven[piece][:, first : first + n, :].rearrange("p c j -> p (c j)"),
             )
 
-        def weave(i, c0, c1):
-            nc.scalar.copy(
-                out=woven[i][:].rearrange("p (c u) -> p c u", u=2)[:, c0:c1, :],
-                in_=picked[i][:].rearrange("p u c -> p c u")[:, c0:c1, :],
-            )
-
-        def product(b, j0, n, bank):
-            acc = psum.tile([P, n], F32, name=f"acc{b}_{j0}", tag=bank)
+        def product(acc, b, j0, n):
             nc.tensor.matmul_mx(
-                out=acc[:],
-                lhsT=w_words[b][:].bitcast(FP4X4),
+                out=acc,
+                lhsT=w_words[:, 2 * P * b : 2 * P * (b + 1)].bitcast(FP4X4),
                 lhsT_scale=w_scale[:, P * b : P * (b + 1)],
                 rhs=codes[:, j0 : j0 + n].bitcast(FP8X4),
                 rhs_scale=scales[:, j0 : j0 + n],
                 start=True,
                 stop=True,
             )
-            return acc
 
         def relu_on_scalar(b, j0, n, acc):
-            nc.scalar.activation(out=y[b][:, j0 : j0 + n], in_=acc[:], func=ACT.Relu)
+            nc.scalar.activation(out=y[b][:, j0 : j0 + n], in_=acc, func=ACT.Relu)
 
-        round_pair(0)
-        for i in range(PIECES):
-            gather_pair(0, i)
-        round_pair(1)
-        for i in range(PIECES - 1):
-            gather_pair(1, i)
-            weave(i, 0, PIECE)
-        gather_pair(1, PIECES - 1)
-        weave(PIECES - 1, 0, PIECE // 2)
-        weave(PIECES - 1, PIECE // 2, PIECE)
+        def relu_on_vector(b, j0, n, acc):
+            nc.vector.tensor_scalar_max(out=y[b][:, j0 : j0 + n], in0=acc, scalar1=0.0)
 
-        j0 = 0
-        for i, n in enumerate(QUANTISED):
-            piece, first = divmod(j0, PIECE)
-            nc.vector.quantize_mx(
-                out=codes[:, j0 : j0 + n].bitcast(FP8X4),
-                scales=scales[:, j0 : j0 + n],
-                in_=woven[piece][:, 2 * first : 2 * (first + n)].bitcast(BF16),
-            )
-            acc = product(0, j0, n, f"bank{i}")
-            if i == RELU_ON_VECTOR:
-                nc.vector.tensor_scalar_max(out=y[0][:, j0 : j0 + n], in0=acc[:], scalar1=0.0)
-            else:
-                relu_on_scalar(0, j0, n, acc)
-            j0 = j0 + n
+        low = [psum.tile([P, 2 * PIECE], F32, name=f"low{b}", tag=f"bank{b}") for b in range(2)]
+        third = psum.tile([P, PIECE], F32, name="third", tag="bank2")
+        fourth = psum.tile([P, PIECE], F32, name="fourth", tag="bank3")
+        high = psum.tile([P, 2 * PIECE], F32, name="high", tag="bank4")
+        place(nc.vector.tensor_copy, 1, 0, PIECE)
+        quantise(0, PIECE)
+        for b in range(2):
+            product(low[b][:, 0:PIECE], b, 0, PIECE)
+        place(nc.vector.tensor_copy, 2, 0, PIECE)
+        quantise(PIECE, PIECE)
+        for b in range(2):
+            product(low[b][:, PIECE : 2 * PIECE], b, PIECE, PIECE)
+        place(nc.scalar.copy, 3, 0, P)
+        place(nc.scalar.copy, 3, P, PIECE)
+        quantise(2 * PIECE, PIECE)
+        product(third[:], 0, 2 * PIECE, PIECE)
+        for h in range(2):
+            quantise(3 * PIECE + h * P, P)
+            product(fourth[:, h * P : (h + 1) * P], 0, 3 * PIECE + h * P, P)
+        product(high[:], 1, 2 * PIECE, 2 * PIECE)
+        relu_on_scalar(0, 0, 2 * PIECE, low[0][:])
+        relu_on_scalar(1, 0, 2 * PIECE, low[1][:])
+        relu_on_vector(0, 2 * PIECE, PIECE, third[:])
+        relu_on_vector(0, 3 * PIECE, PIECE, fourth[:])
 
-        centre = keep.tile([P, V], F32, name="centre", tag="w_words0", align_bytes=64)
-        nc.scalar.activation(out=centre[:], in_=gate_sum[:], func=ACT.Copy, scale=-1.0, bias=1.0)
         factors = (gates[:, 0, :], gates[:, 1, :], centre[:])
-        upper = product(1, S // 2, S // 2, "bank4")
-        lower = product(1, 0, S // 2, "bank2")
-        relu_on_scalar(1, S // 2, S // 2, upper)
-        relu_on_scalar(1, 0, S // 2, lower)
+        columns = (first_cols, None, centre_cols)
+
+        def blocks_of(n):
+            return [slice(c, c + P) for c in range(0, n, P)]
 
         def term(b, d, v0, v1):
             got = keep.tile([P, v1 - v0], F32, name=f"term{b}_{d}_{v0}")
@@ -186,43 +188,72 @@ def tile_picked_grand_relu_e_kernel(
             )
             return got
 
-        def sum_by_transposes(b, v0, v1, bank_there, bank_back, queue):
-            n = v1 - v0
-            blocks = [slice(c, c + P) for c in range(0, n, P)]
-            turned = psum.tile([P, n], F32, name=f"turned{b}_{v0}", tag=bank_there)
-            for d in range(3):
-                got = term(b, d, v0, v1)
-                for c, cols in enumerate(blocks):
-                    nc.tensor.matmul(
-                        turned[:, cols],
-                        got[:, cols],
-                        ident[:],
-                        start=(d == 0 and c == 0),
-                        stop=(d == 2 and c == len(blocks) - 1),
-                        is_transpose=True,
-                    )
-            summed = keep.tile([P, n], F32, name=f"summed{b}_{v0}")
-            nc.scalar.copy(out=summed[:], in_=turned[:])
-            res = keep.tile([P, n], F32, name=f"res{b}_{v0}")
-            back = psum.tile([P, n], F32, name=f"back{b}_{v0}", tag=bank_back)
-            for cols in blocks:
-                nc.tensor.transpose(back[:, cols], summed[:, cols], ident[:])
-            nc.scalar.copy(out=res[:], in_=back[:])
-            queue.dma_start(out=out[P * b : P * (b + 1), v0:v1], in_=res[:])
+        def plain(b, d, v0, v1):
+            got = keep.tile([P, v1 - v0], F32, name=f"plain{b}_{d}_{v0}")
+            nc.scalar.activation(out=got[:], in_=y[b][:].indirect(lists[d][:, v0 // 16 : v1 // 16]), func=ACT.Copy)
+            return got
 
-        sum_by_transposes(0, 0, V // 2, "bank5", "bank6", nc.sync)
-        sum_by_transposes(0, V // 2, V, "bank0", "bank1", nc.sync)
-        sum_by_transposes(1, 0, TURNED_LAST, "bank3", "bank7", nc.scalar)
+        def turn(dst, src, n, first, last):
+            blocks = blocks_of(n)
+            for c, cols in enumerate(blocks):
+                nc.tensor.matmul(
+                    dst[:, cols],
+                    src[:, cols],
+                    ident[:],
+                    start=(first and c == 0),
+                    stop=(last and c == len(blocks) - 1),
+                    is_transpose=True,
+                )
 
-        last = [term(1, d, TURNED_LAST, V) for d in range(3)]
-        halves = [slice(h * HALF_LAST, (h + 1) * HALF_LAST) for h in range(2)]
-        two_terms = []
-        for h, cols in enumerate(halves):
-            part = keep.tile([P, HALF_LAST], F32, name=f"two_terms{h}")
-            nc.vector.tensor_tensor(out=part[:], in0=last[0][:, cols], in1=last[1][:, cols], op=ALU.add)
-            two_terms.append(part)
-        for h, cols in enumerate(halves):
-            res = keep.tile([P, HALF_LAST], F32, name=f"res_last{h}")
-            nc.vector.tensor_tensor(out=res[:], in0=two_terms[h][:], in1=last[2][:, cols], op=ALU.add)
-            v0 = TURNED_LAST + h * HALF_LAST
-            nc.sync.dma_start(out=out[P : 2 * P, v0 : v0 + HALF_LAST], in_=res[:])
+        def copy_out(name, src, n):
+            dst = keep.tile([P, n], F32, name=name)
+            nc.scalar.copy(out=dst[:], in_=src)
+            return dst
+
+        def scale_out(name, src, d, v0, n):
+            dst = keep.tile([P, n], F32, name=name)
+            for c, cols in enumerate(blocks_of(n)):
+                col = v0 // P + c
+                nc.scalar.activation(
+                    out=dst[:, cols], in_=src[:, cols], func=ACT.Copy, scale=columns[d][:, col : col + 1]
+                )
+            return dst
+
+        def both(name, n, in0, in1, op):
+            res = keep.tile([P, n], F32, name=name)
+            nc.vector.tensor_tensor(out=res[:], in0=in0, in1=in1, op=op)
+            return res
+
+        def store(b, v0, n, res, queue):
+            queue.dma_start(out=out[P * b : P * (b + 1), v0 : v0 + n], in_=res[:])
+
+        H = V // 2
+        there = [psum.tile([P, 2, H], F32, name=f"there{h}", tag=f"bank{5 + h}") for h in range(2)]
+        back = [psum.tile([P, H], F32, name=f"back{h}", tag=("bank7", "bank0")[h]) for h in range(2)]
+        last0 = term(0, 1, 0, V)
+        got = []
+        for h in range(2):
+            c = plain(0, 2, h * H, (h + 1) * H)
+            if h == 0:
+                relu_on_scalar(1, 2 * PIECE, 2 * PIECE, high[:])
+            p = plain(0, 0, h * H, (h + 1) * H)
+            turn(there[h][:, 0, :], c, H, True, True)
+            turn(there[h][:, 1, :], p, H, True, True)
+        c1a = term(1, 2, 0, H)
+        p1 = term(1, 0, 0, V)
+        for h in range(2):
+            cs = scale_out(f"cs{h}", there[h][:, 0, :], 2, h * H, H)
+            ps = scale_out(f"ps{h}", there[h][:, 1, :], 0, h * H, H)
+            turn(back[h], cs, H, True, False)
+            turn(back[h], ps, H, False, True)
+            if h == 0:
+                c1b = plain(1, 2, H, V)
+        two_a = both("two_a", H, c1a[:], p1[:, 0:H], ALU.add)
+        t1a = term(1, 1, 0, H)
+        store(0, 0, H, both("res00", H, back[0][:], last0[:, 0:H], ALU.add), nc.sync)
+        store(1, 0, H, both("res10", H, two_a[:], t1a[:], ALU.add), nc.sync)
+        c1b_s = both("c1b_s", H, c1b[:], centre[:, H:V], ALU.mult)
+        t1b = term(1, 1, H, V)
+        two_b = both("two_b", H, c1b_s[:], p1[:, H:V], ALU.add)
+        store(0, H, H, both("res01", H, back[1][:], last0[:, H:V], ALU.add), nc.sync)
+        store(1, H, H, both("res11", H, two_b[:], t1b[:], ALU.add), nc.scalar)

@@ -55,20 +55,20 @@ def tile_picked_grand_relu_e_kernel(
 
         w_words = keep.tile([P, 2 * N], U8, name="w_words", align_bytes=64)
         nc.sync.dma_start(out=w_words[:].bitcast(I32), in_=w1_words[0].bitcast(I32))
+        lists = [None] * 3
+        for d, name, src in ((2, "cen_t", cen), (0, "pos1_t", pos1), (1, "pos2_t", pos2)):
+            lst = keep.tile([P, V // 16], U16, name=name)
+            nc.sync.dma_start(lst[:], src)
+            lists[d] = lst
+        gates = keep.tile([P, 2, V], F32, name="gates")
+        nc.sync.dma_start(out=gates[:], in_=gate.rearrange("d p v -> p d v"))
         w_scale = keep.tile([P, N], U8, name="w_scale", align_bytes=64)
         nc.gpsimd.memset(w_scale[:], 0)
         for q in range(4):
-            nc.sync.dma_start(
+            nc.gpsimd.dma_start(
                 out=w_scale[32 * q : 32 * q + 4, :].bitcast(I32),
                 in_=w1_scales[0, 4 * q : 4 * q + 4, :].bitcast(I32),
             )
-        gates = keep.tile([P, 2, V], F32, name="gates")
-        nc.sync.dma_start(out=gates[:], in_=gate.rearrange("d p v -> p d v"))
-        lists = []
-        for name, src in (("pos1_t", pos1), ("pos2_t", pos2), ("cen_t", cen)):
-            lst = keep.tile([P, V // 16], U16, name=name)
-            nc.sync.dma_start(lst[:], src)
-            lists.append(lst)
 
         gate_turned = psum.tile([P, 2, P], F32, name="gate_turned", tag="bank6")
         nc.tensor.transpose(gate_turned[:, 0, :], gate_rows[:, 0, :], ident[:])
@@ -147,30 +147,34 @@ def tile_picked_grand_relu_e_kernel(
         def relu_on_vector(b, j0, n, acc):
             nc.vector.tensor_scalar_max(out=y[b][:, j0 : j0 + n], in0=acc, scalar1=0.0)
 
-        low = [psum.tile([P, 2 * PIECE], F32, name=f"low{b}", tag=f"bank{b}") for b in range(2)]
+        low = psum.tile([P, 2 * PIECE], F32, name="low", tag="bank0")
+        other_first = psum.tile([P, PIECE], F32, name="other_first", tag="bank1")
         third = psum.tile([P, PIECE], F32, name="third", tag="bank2")
-        fourth = psum.tile([P, PIECE], F32, name="fourth", tag="bank3")
-        high = psum.tile([P, 2 * PIECE], F32, name="high", tag="bank4")
+        fourth = [psum.tile([P, P], F32, name=f"fourth{h}", tag=f"bank{3 + h}") for h in range(2)]
         place(nc.vector.tensor_copy, 1, 0, PIECE)
         quantise(0, PIECE)
-        for b in range(2):
-            product(low[b][:, 0:PIECE], b, 0, PIECE)
+        product(low[:, 0:PIECE], 0, 0, PIECE)
+        product(other_first[:], 1, 0, PIECE)
         place(nc.vector.tensor_copy, 2, 0, PIECE)
         quantise(PIECE, PIECE)
-        for b in range(2):
-            product(low[b][:, PIECE : 2 * PIECE], b, PIECE, PIECE)
+        product(low[:, PIECE : 2 * PIECE], 0, PIECE, PIECE)
+        other_second = psum.tile([P, PIECE], F32, name="other_second", tag="bank5")
+        product(other_second[:], 1, PIECE, PIECE)
         place(nc.scalar.copy, 3, 0, P)
         place(nc.scalar.copy, 3, P, PIECE)
         quantise(2 * PIECE, PIECE)
         product(third[:], 0, 2 * PIECE, PIECE)
         for h in range(2):
             quantise(3 * PIECE + h * P, P)
-            product(fourth[:, h * P : (h + 1) * P], 0, 3 * PIECE + h * P, P)
-        product(high[:], 1, 2 * PIECE, 2 * PIECE)
-        relu_on_scalar(0, 0, 2 * PIECE, low[0][:])
-        relu_on_scalar(1, 0, 2 * PIECE, low[1][:])
+            product(fourth[h][:], 0, 3 * PIECE + h * P, P)
+        relu_on_scalar(0, 0, 2 * PIECE, low[:])
+        relu_on_scalar(1, 0, PIECE, other_first[:])
         relu_on_vector(0, 2 * PIECE, PIECE, third[:])
-        relu_on_vector(0, 3 * PIECE, PIECE, fourth[:])
+        relu_on_vector(0, 3 * PIECE, P, fourth[0][:])
+        relu_on_scalar(0, 3 * PIECE + P, P, fourth[1][:])
+        relu_on_vector(1, PIECE, PIECE, other_second[:])
+        high = psum.tile([P, 2 * PIECE], F32, name="high", tag="bank4")
+        product(high[:], 1, 2 * PIECE, 2 * PIECE)
 
         factors = (gates[:, 0, :], gates[:, 1, :], centre[:])
         columns = (first_cols, None, centre_cols)
@@ -228,32 +232,54 @@ def tile_picked_grand_relu_e_kernel(
             queue.dma_start(out=out[P * b : P * (b + 1), v0 : v0 + n], in_=res[:])
 
         H = V // 2
-        there = [psum.tile([P, 2, H], F32, name=f"there{h}", tag=f"bank{5 + h}") for h in range(2)]
-        back = [psum.tile([P, H], F32, name=f"back{h}", tag=("bank7", "bank0")[h]) for h in range(2)]
-        last0 = term(0, 1, 0, V)
-        got = []
-        for h in range(2):
-            c = plain(0, 2, h * H, (h + 1) * H)
-            if h == 0:
-                relu_on_scalar(1, 2 * PIECE, 2 * PIECE, high[:])
-            p = plain(0, 0, h * H, (h + 1) * H)
-            turn(there[h][:, 0, :], c, H, True, True)
-            turn(there[h][:, 1, :], p, H, True, True)
-        c1a = term(1, 2, 0, H)
-        p1 = term(1, 0, 0, V)
-        for h in range(2):
-            cs = scale_out(f"cs{h}", there[h][:, 0, :], 2, h * H, H)
-            ps = scale_out(f"ps{h}", there[h][:, 1, :], 0, h * H, H)
-            turn(back[h], cs, H, True, False)
-            turn(back[h], ps, H, False, True)
-            if h == 0:
-                c1b = plain(1, 2, H, V)
-        two_a = both("two_a", H, c1a[:], p1[:, 0:H], ALU.add)
-        t1a = term(1, 1, 0, H)
-        store(0, 0, H, both("res00", H, back[0][:], last0[:, 0:H], ALU.add), nc.sync)
-        store(1, 0, H, both("res10", H, two_a[:], t1a[:], ALU.add), nc.sync)
-        c1b_s = both("c1b_s", H, c1b[:], centre[:, H:V], ALU.mult)
-        t1b = term(1, 1, H, V)
-        two_b = both("two_b", H, c1b_s[:], p1[:, H:V], ALU.add)
-        store(0, H, H, both("res01", H, back[1][:], last0[:, H:V], ALU.add), nc.sync)
-        store(1, H, H, both("res11", H, two_b[:], t1b[:], ALU.add), nc.scalar)
+        a_there = psum.tile([P, H], F32, name="a_there", tag="bank6")
+        a_back = psum.tile([P, H], F32, name="a_back", tag="bank3")
+        there = [psum.tile([P, 2, 2, P], F32, name=f"there{d}", tag=("bank7", None, "bank0")[d]) if d != 1 else None for d in range(3)]
+        back = [psum.tile([P, 2, P], F32, name=f"back{k}", tag=("bank1", "bank2")[k]) for k in range(2)]
+        for d in range(3):
+            turn(a_there, term(0, d, 0, H), H, d == 0, d == 2)
+        for b in range(2):
+            for d in (2, 0):
+                got = plain(b, d, H, V)
+                for k in range(2):
+                    nc.tensor.transpose(there[d][:, k, b, :], got[:, k * P : (k + 1) * P], ident[:])
+                if b == 0 and d == 0:
+                    relu_on_scalar(1, 2 * PIECE, 2 * PIECE, high[:])
+        last = keep.tile([P, 2, H], F32, name="last")
+
+        def last_term(b):
+            nc.vector.tensor_tensor(
+                out=last[:, b, :], in0=y[b][:].indirect(lists[1][:, H // 16 : V // 16]), in1=gates[:, 1, H:V], op=ALU.mult
+            )
+
+        last_term(0)
+        a_sum = copy_out("a_sum", a_there[:], H)
+        turn(a_back, a_sum, H, True, True)
+        n_p = term(1, 0, 0, H)
+        n_t = term(1, 1, 0, H)
+        n_c = term(1, 2, 0, H)
+        n_two = both("n_two", H, n_p[:], n_t[:], ALU.add)
+        last_term(1)
+        store(1, 0, H, both("n_res", H, n_two[:], n_c[:], ALU.add), nc.sync)
+        for d in (2, 0):
+            for k in range(2):
+                scaled = keep.tile([P, 2, P], F32, name=f"scaled{k}_{d}")
+                col = H // P + k
+                nc.scalar.activation(
+                    out=scaled[:], in_=there[d][:, k, :, :], func=ACT.Copy, scale=columns[d][:, col : col + 1]
+                )
+                for b in range(2):
+                    nc.tensor.matmul(
+                        back[k][:, b, :],
+                        scaled[:, b, :],
+                        ident[:],
+                        start=(d == 2 and b == 0),
+                        stop=(d == 0 and b == 1),
+                        is_transpose=True,
+                    )
+        store(0, 0, H, copy_out("a_res", a_back[:], H), nc.scalar)
+        out_blocks = out.rearrange("(b p) v -> p b v", p=P)
+        for k in range(2):
+            res = keep.tile([P, 2, P], F32, name=f"res{k}")
+            nc.vector.tensor_tensor(out=res[:], in0=back[k][:], in1=last[:, :, k * P : (k + 1) * P], op=ALU.add)
+            nc.sync.dma_start(out=out_blocks[:, :, H + k * P : H + (k + 1) * P], in_=res[:])

@@ -101,7 +101,10 @@ def tile_picked_grand_relu_e_kernel(
         for j in range(4):
             nc.vector.tensor_copy(out=woven[0][:, :, j], in_=rows[j][:].indirect(entries(0, PIECE)))
             if j < 2:
-                nc.scalar.activation(out=early[:, j, :], in_=rows[j][:].indirect(entries(PIECE, S)), func=ACT.Copy)
+                nc.vector.tensor_copy(out=early[:, j, 0:PIECE], in_=rows[j][:].indirect(entries(PIECE, 2 * PIECE)))
+                nc.scalar.activation(
+                    out=early[:, j, PIECE:], in_=rows[j][:].indirect(entries(2 * PIECE, S)), func=ACT.Copy
+                )
             else:
                 for i in range(1, PIECES):
                     nc.scalar.activation(

@@ -106,7 +106,9 @@ def tile_picked_grand_relu_e_kernel(
                     out=early[:, j, PIECE:], in_=rows[j][:].indirect(entries(2 * PIECE, S)), func=ACT.Copy
                 )
             else:
-                for i in range(1, PIECES):
+                if j == 2:
+                    nc.vector.tensor_copy(out=late[0][:, 0, :], in_=rows[j][:].indirect(entries(PIECE, 2 * PIECE)))
+                for i in range(4 - j, PIECES):
                     nc.scalar.activation(
                         out=late[i - 1][:, j - 2, :],
                         in_=rows[j][:].indirect(entries(i * PIECE, (i + 1) * PIECE)),

@@ -40,6 +40,13 @@ def tile_picked_grand_relu_e_kernel(
             in_=zero[0:first_row, :].to_broadcast([first_row, 2 * P]),
         )
         nc.scalar.dma_start(out=gate_rows[first_row:P, :, :], in_=gate[:, 0, :].rearrange("d (c v) -> c d v", v=P))
+        w_scale = keep.tile([P, N], U8, name="w_scale", align_bytes=64)
+        nc.vector.memset(w_scale[:].bitcast(I32), 0)
+        for q in range(4):
+            nc.scalar.dma_start(
+                out=w_scale[32 * q : 32 * q + 4, :].bitcast(I32),
+                in_=w1_scales[0, 4 * q : 4 * q + 4, :].bitcast(I32),
+            )
         ident = keep.tile([P, P], F32, name="ident")
         make_identity(nc, ident[:])
 
@@ -62,14 +69,6 @@ def tile_picked_grand_relu_e_kernel(
             lists[d] = lst
         gates = keep.tile([P, 2, V], F32, name="gates")
         nc.sync.dma_start(out=gates[:], in_=gate.rearrange("d p v -> p d v"))
-        w_scale = keep.tile([P, N], U8, name="w_scale", align_bytes=64)
-        nc.gpsimd.memset(w_scale[:], 0)
-        for q in range(4):
-            nc.gpsimd.dma_start(
-                out=w_scale[32 * q : 32 * q + 4, :].bitcast(I32),
-                in_=w1_scales[0, 4 * q : 4 * q + 4, :].bitcast(I32),
-            )
-
         gate_turned = psum.tile([P, 2, P], F32, name="gate_turned", tag="bank6")
         nc.tensor.transpose(gate_turned[:, 0, :], gate_rows[:, 0, :], ident[:])
         for d in range(2):
@@ -240,7 +239,7 @@ def tile_picked_grand_relu_e_kernel(
         a_there = psum.tile([P, H], F32, name="a_there", tag="bank6")
         a_back = psum.tile([P, H], F32, name="a_back", tag="bank3")
         there = [psum.tile([P, 2, 2, P], F32, name=f"there{d}", tag=("bank7", None, "bank0")[d]) if d != 1 else None for d in range(3)]
-        back = [psum.tile([P, 2, P], F32, name=f"back{k}", tag=("bank1", "bank2")[k]) for k in range(2)]
+        back = psum.tile([P, 2, P], F32, name="back", tag="bank1")
         for d in range(3):
             turn(a_there, term(0, d, 0, H), H, d == 0, d == 2)
         for b in range(2):
@@ -266,25 +265,35 @@ def tile_picked_grand_relu_e_kernel(
         n_two = both("n_two", H, n_p[:], n_t[:], ALU.add)
         last_term(1)
         store(1, 0, H, both("n_res", H, n_two[:], n_c[:], ALU.add), nc.sync)
-        for d in (2, 0):
-            for k in range(2):
-                scaled = keep.tile([P, 2, P], F32, name=f"scaled{k}_{d}")
-                col = H // P + k
-                nc.scalar.activation(
-                    out=scaled[:], in_=there[d][:, k, :, :], func=ACT.Copy, scale=columns[d][:, col : col + 1]
-                )
-                for b in range(2):
-                    nc.tensor.matmul(
-                        back[k][:, b, :],
-                        scaled[:, b, :],
-                        ident[:],
-                        start=(d == 2 and b == 0),
-                        stop=(d == 0 and b == 1),
-                        is_transpose=True,
-                    )
+
+        def scaled(d, k, b0, b1):
+            dst = keep.tile([P, b1 - b0, P], F32, name=f"scaled{d}_{k}_{b0}")
+            col = H // P + k
+            nc.scalar.activation(
+                out=dst[:], in_=there[d][:, k, b0:b1, :], func=ACT.Copy, scale=columns[d][:, col : col + 1]
+            )
+            return dst
+
+        def turn_back(dst, src, first, final):
+            nc.tensor.matmul(dst, src, ident[:], start=first, stop=final, is_transpose=True)
+
+        back_last = [psum.tile([P, P], F32, name=f"back_last{b}", tag=("bank2", "bank5")[b]) for b in range(2)]
+        got = scaled(2, 0, 0, 2)
+        for b in range(2):
+            turn_back(back[:, b, :], got[:, b, :], b == 0, False)
+        got = scaled(2, 1, 0, 2)
+        for b in range(2):
+            turn_back(back_last[b][:], got[:, b, :], True, False)
+        got = scaled(0, 0, 0, 2)
+        for b in range(2):
+            turn_back(back[:, b, :], got[:, b, :], False, b == 1)
+        got = scaled(0, 1, 0, 2)
+        for b in range(2):
+            turn_back(back_last[b][:], got[:, b, :], False, True)
         store(0, 0, H, copy_out("a_res", a_back[:], H), nc.scalar)
         out_blocks = out.rearrange("(b p) v -> p b v", p=P)
-        for k in range(2):
-            res = keep.tile([P, 2, P], F32, name=f"res{k}")
-            nc.vector.tensor_tensor(out=res[:], in0=back[k][:], in1=last[:, :, k * P : (k + 1) * P], op=ALU.add)
-            nc.sync.dma_start(out=out_blocks[:, :, H + k * P : H + (k + 1) * P], in_=res[:])
+        res = keep.tile([P, 2, P], F32, name="res")
+        nc.vector.tensor_tensor(out=res[:], in0=back[:], in1=last[:, :, 0:P], op=ALU.add)
+        nc.sync.dma_start(out=out_blocks[:, :, H : H + P], in_=res[:])
+        for b in range(2):
+            store(b, V - P, P, both(f"res_last{b}", P, back_last[b][:], last[:, b, P:H], ALU.add), (nc.sync, nc.scalar)[b])

@@ -18,9 +18,12 @@ FP4X4 = mybir.dt.float4_e2m1fn_x4
 ALU = mybir.AluOpType
 ACT = mybir.ActivationFunctionType
 
+ROWS = 4
 PIECE = 256
 PIECES = S // PIECE
-GATE_CHUNKS = V // P
+BLOCKS = V // P
+HALF = V // 2
+POS1, POS2, CEN = 0, 1, 2
 
 
 def tile_picked_grand_relu_e_kernel(
@@ -32,7 +35,7 @@ def tile_picked_grand_relu_e_kernel(
         psum = ctx.enter_context(tc.psum_pool(name="psum", bufs=1))
 
         gate_rows = keep.tile([P, 2, P], F32, name="gate_rows")
-        first_row = P - GATE_CHUNKS
+        first_row = P - BLOCKS
         zero = keep.tile([P, 1], F32, name="zero")
         nc.vector.memset(zero[:], 0.0)
         nc.scalar.copy(
@@ -50,81 +53,75 @@ def tile_picked_grand_relu_e_kernel(
         ident = keep.tile([P, P], F32, name="ident")
         make_identity(nc, ident[:])
 
-        x_rows = xT.rearrange("(p j) t -> p j t", j=4)
+        x_rows = xT.rearrange("(p j) t -> p j t", j=ROWS)
         offs_t = keep.tile([P, S // 16], U16, name="offs_t")
         rows = []
-        for j in range(4):
+        for j in range(ROWS):
             row = keep.tile([P, T], F32, name=f"row{j}")
             nc.sync.dma_start(out=row[:], in_=x_rows[:, j, :])
             rows.append(row)
             if j == 0:
                 nc.sync.dma_start(offs_t[:], offs)
-
         w_words = keep.tile([P, 2 * N], U8, name="w_words", align_bytes=64)
         nc.sync.dma_start(out=w_words[:].bitcast(I32), in_=w1_words[0].bitcast(I32))
-        lists = [None] * 3
-        for d, name, src in ((2, "cen_t", cen), (0, "pos1_t", pos1), (1, "pos2_t", pos2)):
-            lst = keep.tile([P, V // 16], U16, name=name)
-            nc.sync.dma_start(lst[:], src)
-            lists[d] = lst
-        gates = keep.tile([P, 2, V], F32, name="gates")
-        nc.sync.dma_start(out=gates[:], in_=gate.rearrange("d p v -> p d v"))
+        lists = {}
+        for d, name, src in ((CEN, "cen_t", cen), (POS1, "pos1_t", pos1), (POS2, "pos2_t", pos2)):
+            lists[d] = keep.tile([P, V // 16], U16, name=name)
+            nc.sync.dma_start(lists[d][:], src)
+        second_gate = keep.tile([P, V], F32, name="second_gate")
+        nc.sync.dma_start(out=second_gate[:], in_=gate[1])
+
         gate_turned = psum.tile([P, 2, P], F32, name="gate_turned", tag="bank6")
         nc.tensor.transpose(gate_turned[:, 0, :], gate_rows[:, 0, :], ident[:])
         for d in range(2):
             nc.tensor.matmul(
                 gate_turned[:, 1, :], gate_rows[:, d, :], ident[:], start=(d == 0), stop=(d == 1), is_transpose=True
             )
-        first_cols = keep.tile([P, GATE_CHUNKS], F32, name="first_cols")
-        centre_cols = keep.tile([P, GATE_CHUNKS], F32, name="centre_cols")
+        columns = {d: keep.tile([P, BLOCKS], F32, name=f"columns{d}") for d in (POS1, CEN)}
         nc.scalar.activation(
-            out=centre_cols[:], in_=gate_turned[:, 1, first_row:P], func=ACT.Copy, scale=-1.0, bias=1.0
+            out=columns[CEN][:], in_=gate_turned[:, 1, first_row:P], func=ACT.Copy, scale=-1.0, bias=1.0
         )
-        nc.scalar.copy(out=first_cols[:], in_=gate_turned[:, 0, first_row:P])
-        centre_turned = psum.tile([P, V], F32, name="centre_turned", tag="bank7")
-        for c in range(GATE_CHUNKS):
-            nc.tensor.transpose(
-                centre_turned[:, c * P : (c + 1) * P], centre_cols[:, c : c + 1].to_broadcast([P, P]), ident[:]
-            )
-        centre = keep.tile([P, V], F32, name="centre")
-        nc.scalar.copy(out=centre[:], in_=centre_turned[:])
+        nc.scalar.copy(out=columns[POS1][:], in_=gate_turned[:, 0, first_row:P])
+        spread_turned = psum.tile([P, 2, HALF], F32, name="spread_turned", tag="bank7")
+        for slot, d in enumerate((CEN, POS1)):
+            for c in range(HALF // P):
+                nc.tensor.transpose(
+                    spread_turned[:, slot, c * P : (c + 1) * P], columns[d][:, c : c + 1].to_broadcast([P, P]), ident[:]
+                )
+        spread = keep.tile([P, 2, HALF], F32, name="spread")
+        nc.scalar.copy(out=spread[:], in_=spread_turned[:])
+        factors = {CEN: spread[:, 0, :], POS1: spread[:, 1, :], POS2: second_gate[:]}
 
-        woven = [keep.tile([P, PIECE, 4], BF16, name=f"woven{i}", align_bytes=64) for i in range(PIECES)]
+        woven = [keep.tile([P, PIECE, ROWS], BF16, name=f"woven{i}", align_bytes=64) for i in range(PIECES)]
         early = keep.tile([P, 2, S - PIECE], BF16, name="early")
-        late = [keep.tile([P, 2, PIECE], BF16, name=f"late{i}") for i in range(1, PIECES)]
+        late = {i: keep.tile([P, 2, PIECE], BF16, name=f"late{i}") for i in range(1, PIECES)}
         y = [keep.tile([P, S], F32, name=f"y{b}") for b in range(2)]
 
-        def entries(j0, j1):
-            return offs_t[:, j0 // 16 : j1 // 16]
+        def picked(j, i0, i1):
+            return rows[j][:].indirect(offs_t[:, i0 * PIECE // 16 : i1 * PIECE // 16])
 
-        for j in range(4):
-            nc.vector.tensor_copy(out=woven[0][:, :, j], in_=rows[j][:].indirect(entries(0, PIECE)))
-            if j < 2:
-                nc.vector.tensor_copy(out=early[:, j, 0:PIECE], in_=rows[j][:].indirect(entries(PIECE, 2 * PIECE)))
-                nc.scalar.activation(
-                    out=early[:, j, PIECE:], in_=rows[j][:].indirect(entries(2 * PIECE, S)), func=ACT.Copy
-                )
-            else:
-                if j == 2:
-                    nc.vector.tensor_copy(out=late[0][:, 0, :], in_=rows[j][:].indirect(entries(PIECE, 2 * PIECE)))
-                for i in range(4 - j, PIECES):
-                    nc.scalar.activation(
-                        out=late[i - 1][:, j - 2, :],
-                        in_=rows[j][:].indirect(entries(i * PIECE, (i + 1) * PIECE)),
-                        func=ACT.Copy,
-                    )
-            if j == 1:
-                for i in range(1, PIECES):
-                    nc.vector.tensor_copy(
-                        out=woven[i][:, :, 0:2],
-                        in_=early[:, :, (i - 1) * PIECE : i * PIECE].rearrange("p j c -> p c j"),
-                    )
-
-        def place(engine_copy, i, c0, c1):
-            engine_copy(out=woven[i][:, c0:c1, 2:4], in_=late[i - 1][:, :, c0:c1].rearrange("p j c -> p c j"))
+        for j in range(2):
+            nc.vector.tensor_copy(out=woven[0][:, :, j], in_=picked(j, 0, 1))
+            nc.vector.tensor_copy(out=early[:, j, 0:PIECE], in_=picked(j, 1, 2))
+            nc.scalar.activation(out=early[:, j, PIECE:], in_=picked(j, 2, PIECES), func=ACT.Copy)
+        for i in range(1, PIECES):
+            nc.vector.tensor_copy(
+                out=woven[i][:, :, 0:2],
+                in_=early[:, :, (i - 1) * PIECE : i * PIECE].rearrange("p j c -> p c j"),
+            )
+        nc.vector.tensor_copy(out=woven[0][:, :, 2], in_=picked(2, 0, 1))
+        nc.vector.tensor_copy(out=late[1][:, 0, :], in_=picked(2, 1, 2))
+        for i in range(2, PIECES):
+            nc.scalar.activation(out=late[i][:, 0, :], in_=picked(2, i, i + 1), func=ACT.Copy)
+        nc.vector.tensor_copy(out=woven[0][:, :, 3], in_=picked(3, 0, 1))
+        for i in range(1, PIECES):
+            nc.scalar.activation(out=late[i][:, 1, :], in_=picked(3, i, i + 1), func=ACT.Copy)
 
         codes = keep.tile([P, S], U32, name="codes", align_bytes=64)
         scales = keep.tile([P, S], U8, name="scales", align_bytes=64)
+
+        def place(engine_copy, i, c0, c1):
+            engine_copy(out=woven[i][:, c0:c1, 2:4], in_=late[i][:, :, c0:c1].rearrange("p j c -> p c j"))
 
         def quantise(j0, n):
             piece, first = divmod(j0, PIECE)
@@ -151,149 +148,109 @@ def tile_picked_grand_relu_e_kernel(
         def relu_on_vector(b, j0, n, acc):
             nc.vector.tensor_scalar_max(out=y[b][:, j0 : j0 + n], in0=acc, scalar1=0.0)
 
-        low = psum.tile([P, 2 * PIECE], F32, name="low", tag="bank0")
-        other_first = psum.tile([P, PIECE], F32, name="other_first", tag="bank1")
-        third = psum.tile([P, PIECE], F32, name="third", tag="bank2")
-        fourth = [psum.tile([P, P], F32, name=f"fourth{h}", tag=f"bank{3 + h}") for h in range(2)]
+        acc0_01 = psum.tile([P, 2 * PIECE], F32, name="acc0_01", tag="bank0")
+        acc1_0 = psum.tile([P, PIECE], F32, name="acc1_0", tag="bank1")
+        acc0_2 = psum.tile([P, PIECE], F32, name="acc0_2", tag="bank2")
+        acc0_3 = [psum.tile([P, P], F32, name=f"acc0_3{h}", tag=f"bank{3 + h}") for h in range(2)]
         place(nc.vector.tensor_copy, 1, 0, PIECE)
         quantise(0, PIECE)
-        product(low[:, 0:PIECE], 0, 0, PIECE)
-        product(other_first[:], 1, 0, PIECE)
+        product(acc0_01[:, 0:PIECE], 0, 0, PIECE)
+        product(acc1_0[:], 1, 0, PIECE)
         place(nc.vector.tensor_copy, 2, 0, PIECE)
         quantise(PIECE, PIECE)
-        product(low[:, PIECE : 2 * PIECE], 0, PIECE, PIECE)
-        other_second = psum.tile([P, PIECE], F32, name="other_second", tag="bank5")
-        product(other_second[:], 1, PIECE, PIECE)
+        product(acc0_01[:, PIECE : 2 * PIECE], 0, PIECE, PIECE)
+        acc1_1 = psum.tile([P, PIECE], F32, name="acc1_1", tag="bank5")
+        product(acc1_1[:], 1, PIECE, PIECE)
         place(nc.scalar.copy, 3, 0, P)
         place(nc.scalar.copy, 3, P, PIECE)
         quantise(2 * PIECE, PIECE)
-        product(third[:], 0, 2 * PIECE, PIECE)
+        product(acc0_2[:], 0, 2 * PIECE, PIECE)
         for h in range(2):
             quantise(3 * PIECE + h * P, P)
-            product(fourth[h][:], 0, 3 * PIECE + h * P, P)
-        relu_on_scalar(0, 0, 2 * PIECE, low[:])
-        relu_on_scalar(1, 0, PIECE, other_first[:])
-        relu_on_vector(0, 2 * PIECE, PIECE, third[:])
-        relu_on_vector(0, 3 * PIECE, P, fourth[0][:])
-        relu_on_scalar(0, 3 * PIECE + P, P, fourth[1][:])
-        relu_on_vector(1, PIECE, PIECE, other_second[:])
-        high = psum.tile([P, 2 * PIECE], F32, name="high", tag="bank4")
-        product(high[:], 1, 2 * PIECE, 2 * PIECE)
+            product(acc0_3[h][:], 0, 3 * PIECE + h * P, P)
+        relu_on_scalar(0, 0, 2 * PIECE, acc0_01[:])
+        relu_on_scalar(1, 0, PIECE, acc1_0[:])
+        relu_on_vector(0, 2 * PIECE, PIECE, acc0_2[:])
+        relu_on_vector(0, 3 * PIECE, P, acc0_3[0][:])
+        relu_on_scalar(0, 3 * PIECE + P, P, acc0_3[1][:])
+        relu_on_vector(1, PIECE, PIECE, acc1_1[:])
+        acc1_23 = psum.tile([P, 2 * PIECE], F32, name="acc1_23", tag="bank4")
+        product(acc1_23[:], 1, 2 * PIECE, 2 * PIECE)
 
-        factors = (gates[:, 0, :], gates[:, 1, :], centre[:])
-        columns = (first_cols, None, centre_cols)
+        def fetched(b, d, v0, v1):
+            return y[b][:].indirect(lists[d][:, v0 // 16 : v1 // 16])
 
-        def blocks_of(n):
-            return [slice(c, c + P) for c in range(0, n, P)]
+        def weighted(dst, b, d, v0, v1):
+            nc.vector.tensor_tensor(out=dst, in0=fetched(b, d, v0, v1), in1=factors[d][:, v0:v1], op=ALU.mult)
 
-        def term(b, d, v0, v1):
-            got = keep.tile([P, v1 - v0], F32, name=f"term{b}_{d}_{v0}")
-            nc.vector.tensor_tensor(
-                out=got[:],
-                in0=y[b][:].indirect(lists[d][:, v0 // 16 : v1 // 16]),
-                in1=factors[d][:, v0:v1],
-                op=ALU.mult,
-            )
+        def lower_term(b, d):
+            got = keep.tile([P, HALF], F32, name=f"lower{b}_{d}")
+            weighted(got[:], b, d, 0, HALF)
             return got
 
-        def plain(b, d, v0, v1):
-            got = keep.tile([P, v1 - v0], F32, name=f"plain{b}_{d}_{v0}")
-            nc.scalar.activation(out=got[:], in_=y[b][:].indirect(lists[d][:, v0 // 16 : v1 // 16]), func=ACT.Copy)
-            return got
+        def turn(dst, src, first, final):
+            nc.tensor.matmul(dst, src, ident[:], start=first, stop=final, is_transpose=True)
 
-        def turn(dst, src, n, first, last):
-            blocks = blocks_of(n)
-            for c, cols in enumerate(blocks):
-                nc.tensor.matmul(
-                    dst[:, cols],
-                    src[:, cols],
-                    ident[:],
-                    start=(first and c == 0),
-                    stop=(last and c == len(blocks) - 1),
-                    is_transpose=True,
-                )
+        def turn_half(dst, src, first, final):
+            for c in range(HALF // P):
+                cols = slice(c * P, (c + 1) * P)
+                turn(dst[:, cols], src[:, cols], first and c == 0, final and c == HALF // P - 1)
 
-        def copy_out(name, src, n):
-            dst = keep.tile([P, n], F32, name=name)
-            nc.scalar.copy(out=dst[:], in_=src)
+        def copy_out(name, src):
+            dst = keep.tile([P, HALF], F32, name=name)
+            nc.scalar.copy(out=dst[:], in_=src[:])
             return dst
 
-        def scale_out(name, src, d, v0, n):
-            dst = keep.tile([P, n], F32, name=name)
-            for c, cols in enumerate(blocks_of(n)):
-                col = v0 // P + c
-                nc.scalar.activation(
-                    out=dst[:, cols], in_=src[:, cols], func=ACT.Copy, scale=columns[d][:, col : col + 1]
-                )
-            return dst
-
-        def both(name, n, in0, in1, op):
+        def added(name, n, in0, in1):
             res = keep.tile([P, n], F32, name=name)
-            nc.vector.tensor_tensor(out=res[:], in0=in0, in1=in1, op=op)
+            nc.vector.tensor_tensor(out=res[:], in0=in0, in1=in1, op=ALU.add)
             return res
 
         def store(b, v0, n, res, queue):
             queue.dma_start(out=out[P * b : P * (b + 1), v0 : v0 + n], in_=res[:])
 
-        H = V // 2
-        a_there = psum.tile([P, H], F32, name="a_there", tag="bank6")
-        a_back = psum.tile([P, H], F32, name="a_back", tag="bank3")
-        there = [psum.tile([P, 2, 2, P], F32, name=f"there{d}", tag=("bank7", None, "bank0")[d]) if d != 1 else None for d in range(3)]
-        back = psum.tile([P, 2, P], F32, name="back", tag="bank1")
-        for d in range(3):
-            turn(a_there, term(0, d, 0, H), H, d == 0, d == 2)
+        sum_turned = psum.tile([P, HALF], F32, name="sum_turned", tag="bank6")
+        sum_back = psum.tile([P, HALF], F32, name="sum_back", tag="bank3")
+        upper_turned = {
+            d: psum.tile([P, 2, 2, P], F32, name=f"upper_turned{d}", tag=bank)
+            for d, bank in ((POS1, "bank7"), (CEN, "bank0"))
+        }
+        third_back = psum.tile([P, 2, P], F32, name="third_back", tag="bank1")
+        for d in (POS1, POS2, CEN):
+            turn_half(sum_turned, lower_term(0, d), d == POS1, d == CEN)
         for b in range(2):
-            for d in (2, 0):
-                got = plain(b, d, H, V)
+            for d in (CEN, POS1):
+                got = keep.tile([P, HALF], F32, name=f"upper{b}_{d}")
+                nc.scalar.activation(out=got[:], in_=fetched(b, d, HALF, V), func=ACT.Copy)
                 for k in range(2):
-                    nc.tensor.transpose(there[d][:, k, b, :], got[:, k * P : (k + 1) * P], ident[:])
-                if b == 0 and d == 0:
-                    relu_on_scalar(1, 2 * PIECE, 2 * PIECE, high[:])
-        last = keep.tile([P, 2, H], F32, name="last")
+                    nc.tensor.transpose(upper_turned[d][:, k, b, :], got[:, k * P : (k + 1) * P], ident[:])
+            if b == 0:
+                relu_on_scalar(1, 2 * PIECE, 2 * PIECE, acc1_23[:])
+        upper_pos2 = keep.tile([P, 2, HALF], F32, name="upper_pos2")
+        weighted(upper_pos2[:, 0, :], 0, POS2, HALF, V)
+        turn_half(sum_back, copy_out("sum_rows", sum_turned), True, True)
 
-        def last_term(b):
-            nc.vector.tensor_tensor(
-                out=last[:, b, :], in0=y[b][:].indirect(lists[1][:, H // 16 : V // 16]), in1=gates[:, 1, H:V], op=ALU.mult
-            )
+        terms = {d: lower_term(1, d) for d in (POS1, POS2, CEN)}
+        two_terms = added("two_terms", HALF, terms[POS1][:], terms[POS2][:])
+        weighted(upper_pos2[:, 1, :], 1, POS2, HALF, V)
+        store(1, 0, HALF, added("lower_result1", HALF, two_terms[:], terms[CEN][:]), nc.sync)
 
-        last_term(0)
-        a_sum = copy_out("a_sum", a_there[:], H)
-        turn(a_back, a_sum, H, True, True)
-        n_p = term(1, 0, 0, H)
-        n_t = term(1, 1, 0, H)
-        n_c = term(1, 2, 0, H)
-        n_two = both("n_two", H, n_p[:], n_t[:], ALU.add)
-        last_term(1)
-        store(1, 0, H, both("n_res", H, n_two[:], n_c[:], ALU.add), nc.sync)
-
-        def scaled(d, k, b0, b1):
-            dst = keep.tile([P, b1 - b0, P], F32, name=f"scaled{d}_{k}_{b0}")
-            col = H // P + k
-            nc.scalar.activation(
-                out=dst[:], in_=there[d][:, k, b0:b1, :], func=ACT.Copy, scale=columns[d][:, col : col + 1]
-            )
-            return dst
-
-        def turn_back(dst, src, first, final):
-            nc.tensor.matmul(dst, src, ident[:], start=first, stop=final, is_transpose=True)
-
-        back_last = [psum.tile([P, P], F32, name=f"back_last{b}", tag=("bank2", "bank5")[b]) for b in range(2)]
-        got = scaled(2, 0, 0, 2)
-        for b in range(2):
-            turn_back(back[:, b, :], got[:, b, :], b == 0, False)
-        got = scaled(2, 1, 0, 2)
-        for b in range(2):
-            turn_back(back_last[b][:], got[:, b, :], True, False)
-        got = scaled(0, 0, 0, 2)
-        for b in range(2):
-            turn_back(back[:, b, :], got[:, b, :], False, b == 1)
-        got = scaled(0, 1, 0, 2)
-        for b in range(2):
-            turn_back(back_last[b][:], got[:, b, :], False, True)
-        store(0, 0, H, copy_out("a_res", a_back[:], H), nc.scalar)
-        out_blocks = out.rearrange("(b p) v -> p b v", p=P)
-        res = keep.tile([P, 2, P], F32, name="res")
-        nc.vector.tensor_tensor(out=res[:], in0=back[:], in1=last[:, :, 0:P], op=ALU.add)
-        nc.sync.dma_start(out=out_blocks[:, :, H : H + P], in_=res[:])
-        for b in range(2):
-            store(b, V - P, P, both(f"res_last{b}", P, back_last[b][:], last[:, b, P:H], ALU.add), (nc.sync, nc.scalar)[b])
+        last_back = [psum.tile([P, P], F32, name=f"last_back{b}", tag=("bank2", "bank5")[b]) for b in range(2)]
+        for d in (CEN, POS1):
+            for k in range(2):
+                scaled = keep.tile([P, 2, P], F32, name=f"scaled{d}_{k}")
+                block = HALF // P + k
+                nc.scalar.activation(
+                    out=scaled[:], in_=upper_turned[d][:, k, :, :], func=ACT.Copy, scale=columns[d][:, block : block + 1]
+                )
+                for b in range(2):
+                    if k == 0:
+                        turn(third_back[:, b, :], scaled[:, b, :], d == CEN and b == 0, d == POS1 and b == 1)
+                    else:
+                        turn(last_back[b][:], scaled[:, b, :], d == CEN, d == POS1)
+        store(0, 0, HALF, copy_out("lower_result0", sum_back), nc.scalar)
+        third_result = keep.tile([P, 2, P], F32, name="third_result")
+        nc.vector.tensor_tensor(out=third_result[:], in0=third_back[:], in1=upper_pos2[:, :, 0:P], op=ALU.add)
+        nc.sync.dma_start(out=out.rearrange("(b p) v -> p b v", p=P)[:, :, HALF : HALF + P], in_=third_result[:])
+        for b, queue in enumerate((nc.sync, nc.scalar)):
+            store(b, V - P, P, added(f"last_result{b}", P, last_back[b][:], upper_pos2[:, b, P:HALF]), queue)

@@ -77,7 +77,7 @@ def tile_picked_grand_relu_e_kernel(
             nc.tensor.matmul(
                 gate_turned[:, 1, :], gate_rows[:, d, :], ident[:], start=(d == 0), stop=(d == 1), is_transpose=True
             )
-        columns = {d: keep.tile([P, BLOCKS], F32, name=f"columns{d}") for d in (POS1, CEN)}
+        columns = {d: keep.tile([P, BLOCKS], F32, name=f"columns{d}", tag=f"columns{d}") for d in (POS1, CEN)}
         nc.scalar.activation(
             out=columns[CEN][:], in_=gate_turned[:, 1, first_row:P], func=ACT.Copy, scale=-1.0, bias=1.0
         )
@@ -196,8 +196,8 @@ def tile_picked_grand_relu_e_kernel(
                 cols = slice(c * P, (c + 1) * P)
                 turn(dst[:, cols], src[:, cols], first and c == 0, final and c == HALF // P - 1)
 
-        def copy_out(name, src):
-            dst = keep.tile([P, HALF], F32, name=name)
+        def copy_out(name, src, tag):
+            dst = keep.tile([P, HALF], F32, name=name, tag=tag)
             nc.scalar.copy(out=dst[:], in_=src[:])
             return dst
 
@@ -224,11 +224,11 @@ def tile_picked_grand_relu_e_kernel(
                 nc.scalar.activation(out=got[:], in_=fetched(b, d, HALF, V), func=ACT.Copy)
                 for k in range(2):
                     nc.tensor.transpose(upper_turned[d][:, k, b, :], got[:, k * P : (k + 1) * P], ident[:])
-            if b == 0:
-                relu_on_scalar(1, 2 * PIECE, 2 * PIECE, acc1_23[:])
+                if b == 0 and d == CEN:
+                    relu_on_scalar(1, 2 * PIECE, 2 * PIECE, acc1_23[:])
         upper_pos2 = keep.tile([P, 2, HALF], F32, name="upper_pos2")
         weighted(upper_pos2[:, 0, :], 0, POS2, HALF, V)
-        turn_half(sum_back, copy_out("sum_rows", sum_turned), True, True)
+        turn_half(sum_back, copy_out("sum_rows", sum_turned, "sum_rows"), True, True)
 
         terms = {d: lower_term(1, d) for d in (POS1, POS2, CEN)}
         two_terms = added("two_terms", HALF, terms[POS1][:], terms[POS2][:])
@@ -248,7 +248,7 @@ def tile_picked_grand_relu_e_kernel(
                         turn(third_back[:, b, :], scaled[:, b, :], d == CEN and b == 0, d == POS1 and b == 1)
                     else:
                         turn(last_back[b][:], scaled[:, b, :], d == CEN, d == POS1)
-        store(0, 0, HALF, copy_out("lower_result0", sum_back), nc.scalar)
+        store(0, 0, HALF, copy_out("lower_result0", sum_back, f"columns{POS1}"), nc.scalar)
         third_result = keep.tile([P, 2, P], F32, name="third_result")
         nc.vector.tensor_tensor(out=third_result[:], in0=third_back[:], in1=upper_pos2[:, :, 0:P], op=ALU.add)
         nc.sync.dma_start(out=out.rearrange("(b p) v -> p b v", p=P)[:, :, HALF : HALF + P], in_=third_result[:])

@@ -174,7 +174,7 @@ def tile_picked_grand_relu_e_kernel(
         relu_on_vector(0, 3 * PIECE, P, acc0_3[0][:])
         relu_on_scalar(0, 3 * PIECE + P, P, acc0_3[1][:])
         relu_on_vector(1, PIECE, PIECE, acc1_1[:])
-        acc1_23 = psum.tile([P, 2 * PIECE], F32, name="acc1_23", tag="bank4")
+        acc1_23 = psum.tile([P, 2 * PIECE], F32, name="acc1_23", tag="bank7")
         product(acc1_23[:], 1, 2 * PIECE, 2 * PIECE)
 
         def fetched(b, d, v0, v1):
@@ -184,7 +184,7 @@ def tile_picked_grand_relu_e_kernel(
             nc.vector.tensor_tensor(out=dst, in0=fetched(b, d, v0, v1), in1=factors[d][:, v0:v1], op=ALU.mult)
 
         def lower_term(b, d):
-            got = keep.tile([P, HALF], F32, name=f"lower{b}_{d}")
+            got = keep.tile([P, HALF], F32, name=f"lower{b}_{d}", tag=f"lower{b}_{d}")
             weighted(got[:], b, d, 0, HALF)
             return got
 
@@ -202,7 +202,7 @@ def tile_picked_grand_relu_e_kernel(
             return dst
 
         def added(name, n, in0, in1):
-            res = keep.tile([P, n], F32, name=name)
+            res = keep.tile([P, n], F32, name=name, tag=name)
             nc.vector.tensor_tensor(out=res[:], in0=in0, in1=in1, op=ALU.add)
             return res
 
@@ -226,14 +226,15 @@ def tile_picked_grand_relu_e_kernel(
                     nc.tensor.transpose(upper_turned[d][:, k, b, :], got[:, k * P : (k + 1) * P], ident[:])
                 if b == 0 and d == CEN:
                     relu_on_scalar(1, 2 * PIECE, 2 * PIECE, acc1_23[:])
-        upper_pos2 = keep.tile([P, 2, HALF], F32, name="upper_pos2")
-        weighted(upper_pos2[:, 0, :], 0, POS2, HALF, V)
+        upper_pos2 = {1: keep.tile([P, HALF], F32, name="upper_pos2_1")}
         turn_half(sum_back, copy_out("sum_rows", sum_turned, "sum_rows"), True, True)
 
         terms = {d: lower_term(1, d) for d in (POS1, POS2, CEN)}
         two_terms = added("two_terms", HALF, terms[POS1][:], terms[POS2][:])
-        weighted(upper_pos2[:, 1, :], 1, POS2, HALF, V)
+        weighted(upper_pos2[1][:], 1, POS2, HALF, V)
         store(1, 0, HALF, added("lower_result1", HALF, two_terms[:], terms[CEN][:]), nc.sync)
+        upper_pos2[0] = keep.tile([P, HALF], F32, name="upper_pos2_0", tag=f"lower1_{POS1}")
+        weighted(upper_pos2[0][:], 0, POS2, HALF, V)
 
         last_back = [psum.tile([P, P], F32, name=f"last_back{b}", tag=("bank2", "bank5")[b]) for b in range(2)]
         for d in (CEN, POS1):
@@ -248,9 +249,8 @@ def tile_picked_grand_relu_e_kernel(
                         turn(third_back[:, b, :], scaled[:, b, :], d == CEN and b == 0, d == POS1 and b == 1)
                     else:
                         turn(last_back[b][:], scaled[:, b, :], d == CEN, d == POS1)
-        store(0, 0, HALF, copy_out("lower_result0", sum_back, f"columns{POS1}"), nc.scalar)
-        third_result = keep.tile([P, 2, P], F32, name="third_result")
-        nc.vector.tensor_tensor(out=third_result[:], in0=third_back[:], in1=upper_pos2[:, :, 0:P], op=ALU.add)
-        nc.sync.dma_start(out=out.rearrange("(b p) v -> p b v", p=P)[:, :, HALF : HALF + P], in_=third_result[:])
-        for b, queue in enumerate((nc.sync, nc.scalar)):
-            store(b, V - P, P, added(f"last_result{b}", P, last_back[b][:], upper_pos2[:, b, P:HALF]), queue)
+        store(0, 0, HALF, copy_out("lower_result0", sum_back, "lower_result0"), nc.scalar)
+        for b in (1, 0):
+            store(b, HALF, P, added(f"third_result{b}", P, third_back[:, b, :], upper_pos2[b][:, 0:P]), nc.sync)
+        for b, queue in ((0, nc.sync), (1, nc.scalar)):
+            store(b, V - P, P, added(f"last_result{b}", P, last_back[b][:], upper_pos2[b][:, P:HALF]), queue)

@@ -211,9 +211,12 @@ def tile_picked_grand_relu_e_kernel(
 
         sum_turned = psum.tile([P, HALF], F32, name="sum_turned", tag="bank6")
         sum_back = psum.tile([P, HALF], F32, name="sum_back", tag="bank3")
+        last_turned = psum.tile([P, 2, 2, P], F32, name="last_turned", tag="bank7")
         upper_turned = {
-            d: psum.tile([P, 2, 2, P], F32, name=f"upper_turned{d}", tag=bank)
-            for d, bank in ((POS1, "bank7"), (CEN, "bank0"))
+            (CEN, 0): psum.tile([P, 2, P], F32, name="third_turned_cen", tag="bank0")[:],
+            (POS1, 0): psum.tile([P, 2, P], F32, name="third_turned_pos1", tag="bank4")[:],
+            (CEN, 1): last_turned[:, 0, :, :],
+            (POS1, 1): last_turned[:, 1, :, :],
         }
         third_back = psum.tile([P, 2, P], F32, name="third_back", tag="bank1")
         for d in (POS1, POS2, CEN):
@@ -223,11 +226,12 @@ def tile_picked_grand_relu_e_kernel(
                 got = keep.tile([P, HALF], F32, name=f"upper{b}_{d}")
                 nc.scalar.activation(out=got[:], in_=fetched(b, d, HALF, V), func=ACT.Copy)
                 for k in range(2):
-                    nc.tensor.transpose(upper_turned[d][:, k, b, :], got[:, k * P : (k + 1) * P], ident[:])
+                    nc.tensor.transpose(upper_turned[d, k][:, b, :], got[:, k * P : (k + 1) * P], ident[:])
                 if b == 0 and d == CEN:
                     relu_on_scalar(1, 2 * PIECE, 2 * PIECE, acc1_23[:])
         upper_pos2 = {1: keep.tile([P, HALF], F32, name="upper_pos2_1")}
         turn_half(sum_back, copy_out("sum_rows", sum_turned, "sum_rows"), True, True)
+
 
         terms = {d: lower_term(1, d) for d in (POS1, POS2, CEN)}
         two_terms = added("two_terms", HALF, terms[POS1][:], terms[POS2][:])
@@ -237,20 +241,20 @@ def tile_picked_grand_relu_e_kernel(
         weighted(upper_pos2[0][:], 0, POS2, HALF, V)
 
         last_back = [psum.tile([P, P], F32, name=f"last_back{b}", tag=("bank2", "bank5")[b]) for b in range(2)]
-        for d in (CEN, POS1):
-            for k in range(2):
-                scaled = keep.tile([P, 2, P], F32, name=f"scaled{d}_{k}")
+        for k in range(2):
+            for d in (CEN, POS1):
+                scaled = keep.tile([P, 2, P], F32, name=f"scaled{d}_{k}", tag=f"scaled{d}_{k}")
                 block = HALF // P + k
                 nc.scalar.activation(
-                    out=scaled[:], in_=upper_turned[d][:, k, :, :], func=ACT.Copy, scale=columns[d][:, block : block + 1]
+                    out=scaled[:], in_=upper_turned[d, k], func=ACT.Copy, scale=columns[d][:, block : block + 1]
                 )
                 for b in range(2):
                     if k == 0:
                         turn(third_back[:, b, :], scaled[:, b, :], d == CEN and b == 0, d == POS1 and b == 1)
                     else:
                         turn(last_back[b][:], scaled[:, b, :], d == CEN, d == POS1)
-        store(0, 0, HALF, copy_out("lower_result0", sum_back, "lower_result0"), nc.scalar)
+        store(0, 0, HALF, copy_out("lower_result0", sum_back, f"scaled{CEN}_0"), nc.sync)
         for b in (1, 0):
             store(b, HALF, P, added(f"third_result{b}", P, third_back[:, b, :], upper_pos2[b][:, 0:P]), nc.sync)
-        for b, queue in ((0, nc.sync), (1, nc.scalar)):
+        for b, queue in ((0, nc.sync), (1, nc.sync)):
             store(b, V - P, P, added(f"last_result{b}", P, last_back[b][:], upper_pos2[b][:, P:HALF]), queue)

@@ -149,13 +149,14 @@ def tile_picked_grand_relu_e_kernel(
             nc.vector.tensor_scalar_max(out=y[b][:, j0 : j0 + n], in0=acc, scalar1=0.0)
 
         acc0_01 = psum.tile([P, 2 * PIECE], F32, name="acc0_01", tag="bank0")
-        acc1_0 = psum.tile([P, PIECE], F32, name="acc1_0", tag="bank1")
         acc0_2 = psum.tile([P, PIECE], F32, name="acc0_2", tag="bank2")
-        acc0_3 = [psum.tile([P, P], F32, name=f"acc0_3{h}", tag=f"bank{3 + h}") for h in range(2)]
+        shared = psum.tile([P, PIECE + P], F32, name="shared", tag="bank4")
+        acc1_0 = shared[:, 0:PIECE]
+        acc0_3 = [psum.tile([P, P], F32, name="acc0_30", tag="bank3")[:], shared[:, PIECE : PIECE + P]]
         place(nc.vector.tensor_copy, 1, 0, PIECE)
         quantise(0, PIECE)
         product(acc0_01[:, 0:PIECE], 0, 0, PIECE)
-        product(acc1_0[:], 1, 0, PIECE)
+        product(acc1_0, 1, 0, PIECE)
         place(nc.vector.tensor_copy, 2, 0, PIECE)
         quantise(PIECE, PIECE)
         product(acc0_01[:, PIECE : 2 * PIECE], 0, PIECE, PIECE)
@@ -167,12 +168,12 @@ def tile_picked_grand_relu_e_kernel(
         product(acc0_2[:], 0, 2 * PIECE, PIECE)
         for h in range(2):
             quantise(3 * PIECE + h * P, P)
-            product(acc0_3[h][:], 0, 3 * PIECE + h * P, P)
+            product(acc0_3[h], 0, 3 * PIECE + h * P, P)
         relu_on_scalar(0, 0, 2 * PIECE, acc0_01[:])
-        relu_on_scalar(1, 0, PIECE, acc1_0[:])
         relu_on_vector(0, 2 * PIECE, PIECE, acc0_2[:])
-        relu_on_vector(0, 3 * PIECE, P, acc0_3[0][:])
-        relu_on_scalar(0, 3 * PIECE + P, P, acc0_3[1][:])
+        relu_on_vector(0, 3 * PIECE, P, acc0_3[0])
+        relu_on_scalar(0, 3 * PIECE + P, P, acc0_3[1])
+        relu_on_scalar(1, 0, PIECE, acc1_0)
         relu_on_vector(1, PIECE, PIECE, acc1_1[:])
         acc1_23 = psum.tile([P, 2 * PIECE], F32, name="acc1_23", tag="bank7")
         product(acc1_23[:], 1, 2 * PIECE, 2 * PIECE)

@@ -160,8 +160,6 @@ def tile_picked_grand_relu_e_kernel(
         place(nc.vector.tensor_copy, 2, 0, PIECE)
         quantise(PIECE, PIECE)
         product(acc0_01[:, PIECE : 2 * PIECE], 0, PIECE, PIECE)
-        acc1_1 = psum.tile([P, PIECE], F32, name="acc1_1", tag="bank5")
-        product(acc1_1[:], 1, PIECE, PIECE)
         place(nc.scalar.copy, 3, 0, P)
         place(nc.scalar.copy, 3, P, PIECE)
         quantise(2 * PIECE, PIECE)
@@ -174,7 +172,8 @@ def tile_picked_grand_relu_e_kernel(
         relu_on_vector(0, 3 * PIECE, P, acc0_3[0])
         relu_on_scalar(0, 3 * PIECE + P, P, acc0_3[1])
         relu_on_scalar(1, 0, PIECE, acc1_0)
-        relu_on_vector(1, PIECE, PIECE, acc1_1[:])
+        acc1_1 = psum.tile([P, PIECE], F32, name="acc1_1", tag="bank2")
+        product(acc1_1[:], 1, PIECE, PIECE)
         acc1_23 = psum.tile([P, 2 * PIECE], F32, name="acc1_23", tag="bank7")
         product(acc1_23[:], 1, 2 * PIECE, 2 * PIECE)
 
@@ -229,6 +228,7 @@ def tile_picked_grand_relu_e_kernel(
                 for k in range(2):
                     nc.tensor.transpose(upper_turned[d, k][:, b, :], got[:, k * P : (k + 1) * P], ident[:])
                 if b == 0 and d == CEN:
+                    relu_on_scalar(1, PIECE, PIECE, acc1_1[:])
                     relu_on_scalar(1, 2 * PIECE, 2 * PIECE, acc1_23[:])
         upper_pos2 = {1: keep.tile([P, HALF], F32, name="upper_pos2_1")}
         turn_half(sum_back, copy_out("sum_rows", sum_turned, "sum_rows"), True, True)

@@ -150,9 +150,9 @@ def tile_picked_grand_relu_e_kernel(
 
         acc0_01 = psum.tile([P, 2 * PIECE], F32, name="acc0_01", tag="bank0")
         acc0_2 = psum.tile([P, PIECE], F32, name="acc0_2", tag="bank2")
-        shared = psum.tile([P, PIECE + P], F32, name="shared", tag="bank4")
+        shared = psum.tile([P, PIECE + P], F32, name="shared", tag="bank3")
         acc1_0 = shared[:, 0:PIECE]
-        acc0_3 = [psum.tile([P, P], F32, name="acc0_30", tag="bank3")[:], shared[:, PIECE : PIECE + P]]
+        acc0_3 = [shared[:, PIECE : PIECE + P], psum.tile([P, P], F32, name="acc0_31", tag="bank4")[:]]
         place(nc.vector.tensor_copy, 1, 0, PIECE)
         quantise(0, PIECE)
         product(acc0_01[:, 0:PIECE], 0, 0, PIECE)
@@ -171,9 +171,10 @@ def tile_picked_grand_relu_e_kernel(
         relu_on_vector(0, 2 * PIECE, PIECE, acc0_2[:])
         relu_on_vector(0, 3 * PIECE, P, acc0_3[0])
         relu_on_scalar(0, 3 * PIECE + P, P, acc0_3[1])
-        relu_on_scalar(1, 0, PIECE, acc1_0)
+        relu_on_vector(1, 0, PIECE, acc1_0)
         acc1_1 = psum.tile([P, PIECE], F32, name="acc1_1", tag="bank2")
         product(acc1_1[:], 1, PIECE, PIECE)
+        relu_on_scalar(1, PIECE, PIECE, acc1_1[:])
         acc1_23 = psum.tile([P, 2 * PIECE], F32, name="acc1_23", tag="bank7")
         product(acc1_23[:], 1, 2 * PIECE, 2 * PIECE)
 
@@ -228,7 +229,6 @@ def tile_picked_grand_relu_e_kernel(
                 for k in range(2):
                     nc.tensor.transpose(upper_turned[d, k][:, b, :], got[:, k * P : (k + 1) * P], ident[:])
                 if b == 0 and d == CEN:
-                    relu_on_scalar(1, PIECE, PIECE, acc1_1[:])
                     relu_on_scalar(1, 2 * PIECE, 2 * PIECE, acc1_23[:])
         upper_pos2 = {1: keep.tile([P, HALF], F32, name="upper_pos2_1")}
         turn_half(sum_back, copy_out("sum_rows", sum_turned, "sum_rows"), True, True)

@@ -94,8 +94,8 @@ def tile_picked_grand_relu_e_kernel(
 
         woven = [keep.tile([P, PIECE, ROWS], BF16, name=f"woven{i}", align_bytes=64) for i in range(PIECES)]
         early = keep.tile([P, 2, S - PIECE], BF16, name="early")
-        late = {i: keep.tile([P, 2, PIECE], BF16, name=f"late{i}") for i in range(1, PIECES)}
-        y = [keep.tile([P, S], F32, name=f"y{b}") for b in range(2)]
+        late = {i: keep.tile([P, 2, PIECE], BF16, name=f"late{i}", tag=f"late{i}") for i in range(1, PIECES)}
+        y = [keep.tile([P, S], F32, name="y0")]
 
         def picked(j, i0, i1):
             return rows[j][:].indirect(offs_t[:, i0 * PIECE // 16 : i1 * PIECE // 16])
@@ -150,9 +150,8 @@ def tile_picked_grand_relu_e_kernel(
 
         acc0_01 = psum.tile([P, 2 * PIECE], F32, name="acc0_01", tag="bank0")
         acc0_2 = psum.tile([P, PIECE], F32, name="acc0_2", tag="bank2")
-        shared = psum.tile([P, PIECE + P], F32, name="shared", tag="bank3")
-        acc1_0 = shared[:, 0:PIECE]
-        acc0_3 = [shared[:, PIECE : PIECE + P], psum.tile([P, P], F32, name="acc0_31", tag="bank4")[:]]
+        acc1_0 = psum.tile([P, PIECE], F32, name="acc1_0", tag="bank5")[:]
+        acc0_3 = [psum.tile([P, P], F32, name=f"acc0_3{h}", tag=("bank3", "bank4")[h])[:] for h in range(2)]
         place(nc.vector.tensor_copy, 1, 0, PIECE)
         quantise(0, PIECE)
         product(acc0_01[:, 0:PIECE], 0, 0, PIECE)
@@ -167,11 +166,12 @@ def tile_picked_grand_relu_e_kernel(
         for h in range(2):
             quantise(3 * PIECE + h * P, P)
             product(acc0_3[h], 0, 3 * PIECE + h * P, P)
+        y.append(keep.tile([P, S], F32, name="y1", tag=f"late{PIECES - 1}"))
+        relu_on_vector(1, 0, PIECE, acc1_0)
         relu_on_scalar(0, 0, 2 * PIECE, acc0_01[:])
         relu_on_vector(0, 2 * PIECE, PIECE, acc0_2[:])
         relu_on_vector(0, 3 * PIECE, P, acc0_3[0])
         relu_on_scalar(0, 3 * PIECE + P, P, acc0_3[1])
-        relu_on_vector(1, 0, PIECE, acc1_0)
         acc1_1 = psum.tile([P, PIECE], F32, name="acc1_1", tag="bank2")
         product(acc1_1[:], 1, PIECE, PIECE)
         relu_on_scalar(1, PIECE, PIECE, acc1_1[:])

@@ -92,10 +92,10 @@ def tile_picked_grand_relu_e_kernel(
         nc.scalar.copy(out=spread[:], in_=spread_turned[:])
         factors = {CEN: spread[:, 0, :], POS1: spread[:, 1, :], POS2: second_gate[:]}
 
-        woven = [keep.tile([P, PIECE, ROWS], BF16, name=f"woven{i}", align_bytes=64) for i in range(PIECES)]
+        woven = [keep.tile([P, PIECE, ROWS], BF16, name=f"woven{i}", tag=f"woven{i}", align_bytes=64) for i in range(PIECES)]
         early = keep.tile([P, 2, S - PIECE], BF16, name="early")
         late = {i: keep.tile([P, 2, PIECE], BF16, name=f"late{i}", tag=f"late{i}") for i in range(1, PIECES)}
-        y = [keep.tile([P, S], F32, name="y0")]
+        y = []
 
         def picked(j, i0, i1):
             return rows[j][:].indirect(offs_t[:, i0 * PIECE // 16 : i1 * PIECE // 16])
@@ -114,8 +114,15 @@ def tile_picked_grand_relu_e_kernel(
         for i in range(2, PIECES):
             nc.scalar.activation(out=late[i][:, 0, :], in_=picked(2, i, i + 1), func=ACT.Copy)
         nc.vector.tensor_copy(out=woven[0][:, :, 3], in_=picked(3, 0, 1))
-        for i in range(1, PIECES):
+        for i in range(1, PIECES - 1):
             nc.scalar.activation(out=late[i][:, 1, :], in_=picked(3, i, i + 1), func=ACT.Copy)
+        for h in range(2):
+            first = S - PIECE + h * P
+            nc.scalar.activation(
+                out=late[PIECES - 1][:, 1, h * P : (h + 1) * P],
+                in_=rows[3][:].indirect(offs_t[:, first // 16 : (first + P) // 16]),
+                func=ACT.Copy,
+            )
 
         codes = keep.tile([P, S], U32, name="codes", align_bytes=64)
         scales = keep.tile([P, S], U8, name="scales", align_bytes=64)
@@ -148,17 +155,18 @@ def tile_picked_grand_relu_e_kernel(
         def relu_on_vector(b, j0, n, acc):
             nc.vector.tensor_scalar_max(out=y[b][:, j0 : j0 + n], in0=acc, scalar1=0.0)
 
-        acc0_01 = psum.tile([P, 2 * PIECE], F32, name="acc0_01", tag="bank0")
+        acc0_0 = psum.tile([P, PIECE], F32, name="acc0_0", tag="bank0")
+        acc0_1 = psum.tile([P, PIECE], F32, name="acc0_1", tag="bank1")
         acc0_2 = psum.tile([P, PIECE], F32, name="acc0_2", tag="bank2")
         acc1_0 = psum.tile([P, PIECE], F32, name="acc1_0", tag="bank5")[:]
         acc0_3 = [psum.tile([P, P], F32, name=f"acc0_3{h}", tag=("bank3", "bank4")[h])[:] for h in range(2)]
         place(nc.vector.tensor_copy, 1, 0, PIECE)
         quantise(0, PIECE)
-        product(acc0_01[:, 0:PIECE], 0, 0, PIECE)
+        product(acc0_0[:], 0, 0, PIECE)
         product(acc1_0, 1, 0, PIECE)
         place(nc.vector.tensor_copy, 2, 0, PIECE)
         quantise(PIECE, PIECE)
-        product(acc0_01[:, PIECE : 2 * PIECE], 0, PIECE, PIECE)
+        product(acc0_1[:], 0, PIECE, PIECE)
         place(nc.scalar.copy, 3, 0, P)
         place(nc.scalar.copy, 3, P, PIECE)
         quantise(2 * PIECE, PIECE)
@@ -166,11 +174,13 @@ def tile_picked_grand_relu_e_kernel(
         for h in range(2):
             quantise(3 * PIECE + h * P, P)
             product(acc0_3[h], 0, 3 * PIECE + h * P, P)
+        y.append(keep.tile([P, S], F32, name="y0", tag="woven2", align_bytes=64))
         y.append(keep.tile([P, S], F32, name="y1", tag=f"late{PIECES - 1}"))
         relu_on_vector(1, 0, PIECE, acc1_0)
-        relu_on_scalar(0, 0, 2 * PIECE, acc0_01[:])
+        relu_on_scalar(0, 0, PIECE, acc0_0[:])
+        relu_on_scalar(0, PIECE, PIECE, acc0_1[:])
         relu_on_vector(0, 2 * PIECE, PIECE, acc0_2[:])
-        relu_on_vector(0, 3 * PIECE, P, acc0_3[0])
+        relu_on_scalar(0, 3 * PIECE, P, acc0_3[0])
         relu_on_scalar(0, 3 * PIECE + P, P, acc0_3[1])
         acc1_1 = psum.tile([P, PIECE], F32, name="acc1_1", tag="bank2")
         product(acc1_1[:], 1, PIECE, PIECE)

from contextlib import ExitStack

import concourse.mybir as mybir
from concourse.masks import make_identity

K, T, S, V, N = 512, 2048, 1024, 512, 256
P = 128
FLOPS = 2 * K * S * N

F32 = mybir.dt.float32
BF16 = mybir.dt.bfloat16
I32 = mybir.dt.int32
U32 = mybir.dt.uint32
U16 = mybir.dt.uint16
U8 = mybir.dt.uint8
FP8X4 = mybir.dt.float8_e4m3fn_x4
FP4X4 = mybir.dt.float4_e2m1fn_x4
ALU = mybir.AluOpType
ACT = mybir.ActivationFunctionType

ROWS = 4
PIECE = 256
PIECES = S // PIECE
BLOCKS = V // P
HALF = V // 2
POS1, POS2, CEN = 0, 1, 2


def tile_picked_grand_relu_e_kernel(
    tc, xT, w1_words, w1_scales, gate, offs, cen, pos1, pos2, out
):
    nc = tc.nc
    with ExitStack() as ctx:
        keep = ctx.enter_context(tc.tile_pool(name="keep", bufs=1))
        psum = ctx.enter_context(tc.psum_pool(name="psum", bufs=1))

        gate_rows = keep.tile([P, 2, P], F32, name="gate_rows")
        first_row = P - BLOCKS
        zero = keep.tile([P, 1], F32, name="zero")
        nc.vector.memset(zero[:], 0.0)
        nc.scalar.copy(
            out=gate_rows[0:first_row, :, :].rearrange("p d v -> p (d v)"),
            in_=zero[0:first_row, :].to_broadcast([first_row, 2 * P]),
        )
        nc.scalar.dma_start(out=gate_rows[first_row:P, :, :], in_=gate[:, 0, :].rearrange("d (c v) -> c d v", v=P))
        w_scale = keep.tile([P, N], U8, name="w_scale", align_bytes=64)
        nc.vector.memset(w_scale[:].bitcast(I32), 0)
        for q in range(4):
            nc.scalar.dma_start(
                out=w_scale[32 * q : 32 * q + 4, :].bitcast(I32),
                in_=w1_scales[0, 4 * q : 4 * q + 4, :].bitcast(I32),
            )
        ident = keep.tile([P, P], F32, name="ident")
        make_identity(nc, ident[:])

        x_rows = xT.rearrange("(p j) t -> p j t", j=ROWS)
        offs_t = keep.tile([P, S // 16], U16, name="offs_t")
        rows = []
        for j in range(ROWS):
            row = keep.tile([P, T], F32, name=f"row{j}")
            nc.sync.dma_start(out=row[:], in_=x_rows[:, j, :])
            rows.append(row)
            if j == 0:
                nc.sync.dma_start(offs_t[:], offs)
        w_words = keep.tile([P, 2 * N], U8, name="w_words", align_bytes=64)
        nc.sync.dma_start(out=w_words[:].bitcast(I32), in_=w1_words[0].bitcast(I32))
        lists = {}
        for d, name, src in ((CEN, "cen_t", cen), (POS1, "pos1_t", pos1), (POS2, "pos2_t", pos2)):
            lists[d] = keep.tile([P, V // 16], U16, name=name)
            nc.sync.dma_start(lists[d][:], src)
        second_gate = keep.tile([P, V], F32, name="second_gate")
        nc.sync.dma_start(out=second_gate[:], in_=gate[1])

        gate_turned = psum.tile([P, 2, P], F32, name="gate_turned", tag="bank6")
        nc.tensor.transpose(gate_turned[:, 0, :], gate_rows[:, 0, :], ident[:])
        for d in range(2):
            nc.tensor.matmul(
                gate_turned[:, 1, :], gate_rows[:, d, :], ident[:], start=(d == 0), stop=(d == 1), is_transpose=True
            )
        columns = {d: keep.tile([P, BLOCKS], F32, name=f"columns{d}", tag=f"columns{d}") for d in (POS1, CEN)}
        nc.scalar.activation(
            out=columns[CEN][:], in_=gate_turned[:, 1, first_row:P], func=ACT.Copy, scale=-1.0, bias=1.0
        )
        nc.scalar.copy(out=columns[POS1][:], in_=gate_turned[:, 0, first_row:P])
        spread_turned = psum.tile([P, 2, HALF], F32, name="spread_turned", tag="bank7")
        for slot, d in enumerate((CEN, POS1)):
            for c in range(HALF // P):
                nc.tensor.transpose(
                    spread_turned[:, slot, c * P : (c + 1) * P], columns[d][:, c : c + 1].to_broadcast([P, P]), ident[:]
                )
        spread = keep.tile([P, 2, HALF], F32, name="spread")
        nc.scalar.copy(out=spread[:], in_=spread_turned[:])
        factors = {CEN: spread[:, 0, :], POS1: spread[:, 1, :], POS2: second_gate[:]}

        woven = [keep.tile([P, PIECE, ROWS], BF16, name=f"woven{i}", tag=f"woven{i}", align_bytes=64) for i in range(PIECES)]
        early = keep.tile([P, 2, S - PIECE], BF16, name="early")
        late = {i: keep.tile([P, 2, PIECE], BF16, name=f"late{i}", tag=f"late{i}") for i in range(1, PIECES)}
        y = []

        def picked(j, i0, i1):
            return rows[j][:].indirect(offs_t[:, i0 * PIECE // 16 : i1 * PIECE // 16])

        for j in range(2):
            nc.vector.tensor_copy(out=woven[0][:, :, j], in_=picked(j, 0, 1))
            nc.vector.tensor_copy(out=early[:, j, 0:PIECE], in_=picked(j, 1, 2))
            nc.scalar.activation(out=early[:, j, PIECE:], in_=picked(j, 2, PIECES), func=ACT.Copy)
        for i in range(1, PIECES):
            nc.vector.tensor_copy(
                out=woven[i][:, :, 0:2],
                in_=early[:, :, (i - 1) * PIECE : i * PIECE].rearrange("p j c -> p c j"),
            )
        nc.vector.tensor_copy(out=woven[0][:, :, 2], in_=picked(2, 0, 1))
        nc.vector.tensor_copy(out=late[1][:, 0, :], in_=picked(2, 1, 2))
        for i in range(2, PIECES):
            nc.scalar.activation(out=late[i][:, 0, :], in_=picked(2, i, i + 1), func=ACT.Copy)
        nc.vector.tensor_copy(out=woven[0][:, :, 3], in_=picked(3, 0, 1))
        for i in range(1, PIECES - 1):
            nc.scalar.activation(out=late[i][:, 1, :], in_=picked(3, i, i + 1), func=ACT.Copy)
        for h in range(2):
            first = S - PIECE + h * P
            nc.scalar.activation(
                out=late[PIECES - 1][:, 1, h * P : (h + 1) * P],
                in_=rows[3][:].indirect(offs_t[:, first // 16 : (first + P) // 16]),
                func=ACT.Copy,
            )

        codes = keep.tile([P, S], U32, name="codes", align_bytes=64)
        scales = keep.tile([P, S], U8, name="scales", align_bytes=64)

        def place(engine_copy, i, c0, c1):
            engine_copy(out=woven[i][:, c0:c1, 2:4], in_=late[i][:, :, c0:c1].rearrange("p j c -> p c j"))

        def quantise(j0, n):
            piece, first = divmod(j0, PIECE)
            nc.vector.quantize_mx(
                out=codes[:, j0 : j0 + n].bitcast(FP8X4),
                scales=scales[:, j0 : j0 + n],
                in_=woven[piece][:, first : first + n, :].rearrange("p c j -> p (c j)"),
            )

        def product(acc, b, j0, n):
            nc.tensor.matmul_mx(
                out=acc,
                lhsT=w_words[:, 2 * P * b : 2 * P * (b + 1)].bitcast(FP4X4),
                lhsT_scale=w_scale[:, P * b : P * (b + 1)],
                rhs=codes[:, j0 : j0 + n].bitcast(FP8X4),
                rhs_scale=scales[:, j0 : j0 + n],
                start=True,
                stop=True,
            )

        def relu_on_scalar(b, j0, n, acc):
            nc.scalar.activation(out=y[b][:, j0 : j0 + n], in_=acc, func=ACT.Relu)

        def relu_on_vector(b, j0, n, acc):
            nc.vector.tensor_scalar_max(out=y[b][:, j0 : j0 + n], in0=acc, scalar1=0.0)

        acc0_0 = psum.tile([P, PIECE], F32, name="acc0_0", tag="bank0")
        acc0_1 = psum.tile([P, PIECE], F32, name="acc0_1", tag="bank1")
        acc0_2 = psum.tile([P, PIECE], F32, name="acc0_2", tag="bank2")
        acc1_0 = psum.tile([P, PIECE], F32, name="acc1_0", tag="bank5")[:]
        acc0_3 = [psum.tile([P, P], F32, name=f"acc0_3{h}", tag=("bank3", "bank4")[h])[:] for h in range(2)]
        place(nc.vector.tensor_copy, 1, 0, PIECE)
        quantise(0, PIECE)
        product(acc0_0[:], 0, 0, PIECE)
        product(acc1_0, 1, 0, PIECE)
        place(nc.vector.tensor_copy, 2, 0, PIECE)
        quantise(PIECE, PIECE)
        product(acc0_1[:], 0, PIECE, PIECE)
        place(nc.scalar.copy, 3, 0, P)
        place(nc.scalar.copy, 3, P, PIECE)
        quantise(2 * PIECE, PIECE)
        product(acc0_2[:], 0, 2 * PIECE, PIECE)
        for h in range(2):
            quantise(3 * PIECE + h * P, P)
            product(acc0_3[h], 0, 3 * PIECE + h * P, P)
        y.append(keep.tile([P, S], F32, name="y0", tag="woven2", align_bytes=64))
        y.append(keep.tile([P, S], F32, name="y1", tag=f"late{PIECES - 1}"))
        relu_on_vector(1, 0, PIECE, acc1_0)
        relu_on_scalar(0, 0, PIECE, acc0_0[:])
        relu_on_scalar(0, PIECE, PIECE, acc0_1[:])
        relu_on_vector(0, 2 * PIECE, PIECE, acc0_2[:])
        relu_on_scalar(0, 3 * PIECE, P, acc0_3[0])
        relu_on_scalar(0, 3 * PIECE + P, P, acc0_3[1])
        acc1_1 = psum.tile([P, PIECE], F32, name="acc1_1", tag="bank2")
        product(acc1_1[:], 1, PIECE, PIECE)
        relu_on_scalar(1, PIECE, PIECE, acc1_1[:])
        acc1_23 = psum.tile([P, 2 * PIECE], F32, name="acc1_23", tag="bank7")
        product(acc1_23[:], 1, 2 * PIECE, 2 * PIECE)

        def fetched(b, d, v0, v1):
            return y[b][:].indirect(lists[d][:, v0 // 16 : v1 // 16])

        def weighted(dst, b, d, v0, v1):
            nc.vector.tensor_tensor(out=dst, in0=fetched(b, d, v0, v1), in1=factors[d][:, v0:v1], op=ALU.mult)

        def lower_term(b, d):
            got = keep.tile([P, HALF], F32, name=f"lower{b}_{d}", tag=f"lower{b}_{d}")
            weighted(got[:], b, d, 0, HALF)
            return got

        def turn(dst, src, first, final):
            nc.tensor.matmul(dst, src, ident[:], start=first, stop=final, is_transpose=True)

        def turn_half(dst, src, first, final):
            for c in range(HALF // P):
                cols = slice(c * P, (c + 1) * P)
                turn(dst[:, cols], src[:, cols], first and c == 0, final and c == HALF // P - 1)

        def copy_out(name, src, tag):
            dst = keep.tile([P, HALF], F32, name=name, tag=tag)
            nc.scalar.copy(out=dst[:], in_=src[:])
            return dst

        def added(name, n, in0, in1):
            res = keep.tile([P, n], F32, name=name, tag=name)
            nc.vector.tensor_tensor(out=res[:], in0=in0, in1=in1, op=ALU.add)
            return res

        def store(b, v0, n, res, queue):
            queue.dma_start(out=out[P * b : P * (b + 1), v0 : v0 + n], in_=res[:])

        sum_turned = psum.tile([P, HALF], F32, name="sum_turned", tag="bank6")
        sum_back = psum.tile([P, HALF], F32, name="sum_back", tag="bank3")
        last_turned = psum.tile([P, 2, 2, P], F32, name="last_turned", tag="bank7")
        upper_turned = {
            (CEN, 0): psum.tile([P, 2, P], F32, name="third_turned_cen", tag="bank0")[:],
            (POS1, 0): psum.tile([P, 2, P], F32, name="third_turned_pos1", tag="bank4")[:],
            (CEN, 1): last_turned[:, 0, :, :],
            (POS1, 1): last_turned[:, 1, :, :],
        }
        third_back = psum.tile([P, 2, P], F32, name="third_back", tag="bank1")
        for d in (POS1, POS2, CEN):
            turn_half(sum_turned, lower_term(0, d), d == POS1, d == CEN)
        for b in range(2):
            for d in (CEN, POS1):
                got = keep.tile([P, HALF], F32, name=f"upper{b}_{d}")
                nc.scalar.activation(out=got[:], in_=fetched(b, d, HALF, V), func=ACT.Copy)
                for k in range(2):
                    nc.tensor.transpose(upper_turned[d, k][:, b, :], got[:, k * P : (k + 1) * P], ident[:])
                if b == 0 and d == CEN:
                    relu_on_scalar(1, 2 * PIECE, 2 * PIECE, acc1_23[:])
        upper_pos2 = {1: keep.tile([P, HALF], F32, name="upper_pos2_1")}
        turn_half(sum_back, copy_out("sum_rows", sum_turned, "sum_rows"), True, True)


        terms = {d: lower_term(1, d) for d in (POS1, POS2, CEN)}
        two_terms = added("two_terms", HALF, terms[POS1][:], terms[POS2][:])
        weighted(upper_pos2[1][:], 1, POS2, HALF, V)
        store(1, 0, HALF, added("lower_result1", HALF, two_terms[:], terms[CEN][:]), nc.sync)
        upper_pos2[0] = keep.tile([P, HALF], F32, name="upper_pos2_0", tag=f"lower1_{POS1}")
        weighted(upper_pos2[0][:], 0, POS2, HALF, V)

        last_back = [psum.tile([P, P], F32, name=f"last_back{b}", tag=("bank2", "bank5")[b]) for b in range(2)]
        for k in range(2):
            for d in (CEN, POS1):
                scaled = keep.tile([P, 2, P], F32, name=f"scaled{d}_{k}", tag=f"scaled{d}_{k}")
                block = HALF // P + k
                nc.scalar.activation(
                    out=scaled[:], in_=upper_turned[d, k], func=ACT.Copy, scale=columns[d][:, block : block + 1]
                )
                for b in range(2):
                    if k == 0:
                        turn(third_back[:, b, :], scaled[:, b, :], d == CEN and b == 0, d == POS1 and b == 1)
                    else:
                        turn(last_back[b][:], scaled[:, b, :], d == CEN, d == POS1)
        store(0, 0, HALF, copy_out("lower_result0", sum_back, f"scaled{CEN}_0"), nc.sync)
        for b in (1, 0):
            store(b, HALF, P, added(f"third_result{b}", P, third_back[:, b, :], upper_pos2[b][:, 0:P]), nc.sync)
        for b, queue in ((0, nc.sync), (1, nc.sync)):
            store(b, V - P, P, added(f"last_result{b}", P, last_back[b][:], upper_pos2[b][:, P:HALF]), queue)
